import numpy as np
import ml_dtypes


def mxq(x, axis, fmt="e4m3"):
    dtype, down = {"e4m3": (ml_dtypes.float8_e4m3fn, 7), "e5m2": (ml_dtypes.float8_e5m2, 14)}[fmt]
    v = np.moveaxis(np.asarray(x, np.float32).astype(ml_dtypes.bfloat16).astype(np.float64), axis, -1)
    blocks = v.reshape(v.shape[:-1] + (-1, 32))
    amax = np.abs(blocks).max(-1, keepdims=True)
    byte = np.maximum(np.where(amax > 0, np.frexp(amax)[1] - 1 + 127, 0) - down, 1)
    scale = np.exp2(byte - 127.0)
    codes = (blocks / scale).astype(np.float32).astype(dtype).astype(np.float64)
    return np.moveaxis((codes * scale).reshape(v.shape), -1, axis)


WIDE = False


def mx_kscale(k):
    if not WIDE:
        return np.ones(k)
    levels = np.array([10, -10, 5, -5, 0])
    if k % 512:
        return np.exp2(np.random.permutation(np.resize(levels, k // 32))).repeat(32)
    a = np.empty((k // 512, 16))
    for p in range(k // 512):
        a[p, :8] = np.random.permutation(np.resize(levels, 8))
        for g in range(8):
            far = levels[np.abs(levels - a[p, g]) >= 10]
            a[p, g + 8] = far[np.random.randint(len(far))]
    return np.exp2(a.ravel()).repeat(32)


def f64(x):
    return np.asarray(x).astype(np.float64)


def striped(idx):
    return np.tile(np.asarray(idx).reshape(-1, 16).T, (8, 1)).astype(np.uint16)


def unstriped(offs):
    return offs[:16].T.reshape(-1).astype(np.int64)


E2M1 = np.array([0.0, 0.5, 1.0, 1.5, 2.0, 3.0, 4.0, 6.0, -0.0, -0.5, -1.0, -1.5, -2.0, -3.0, -4.0, -6.0])


def pack_weight(w, fmt):
    k, n = w.shape
    w = f64(np.asarray(w, np.float32).astype(ml_dtypes.bfloat16)).reshape(k // 32, 32, n)
    amax = np.abs(w).max(1)
    if fmt == "e4m3":
        byte = np.frexp(amax)[1] - 1 + 127 - 7
    else:
        mant, ex = np.frexp(amax / 6.0)
        byte = np.where(mant > 0.5, ex, ex - 1) + 127
    byte = np.clip(np.where(amax > 0, byte, 1), 1, 254)
    scaled = (w * np.exp2(127.0 - byte)[:, None, :]).reshape(k, n).astype(np.float32)
    by_word = np.ascontiguousarray(scaled.reshape(k // 512, 128, 4, n).transpose(0, 1, 3, 2))
    if fmt == "e4m3":
        words = by_word.astype(ml_dtypes.float8_e4m3fn).view(np.uint8)
    else:
        c = by_word.astype(ml_dtypes.float4_e2m1fn).view(np.uint8) & 0xF
        words = (c[..., 0::2] | (c[..., 1::2] << 4)).reshape(k // 512, 128, 2 * n)
    return np.ascontiguousarray(words), np.ascontiguousarray(byte.astype(np.uint8).reshape(k // 512, 16, n))


def unpack_weight(words, scales, fmt):
    g, _, n = scales.shape
    words = np.ascontiguousarray(words).reshape(g, 128, n, -1)
    if fmt == "e4m3":
        vals = words.view(ml_dtypes.float8_e4m3fn).astype(np.float64)
    else:
        nib = np.empty((g, 128, n, 4), np.uint8)
        nib[..., 0::2] = words & 0xF
        nib[..., 1::2] = words >> 4
        vals = E2M1[nib]
    vals = vals * np.repeat(np.exp2(scales.astype(np.float64) - 127.0), 8, axis=1)[..., None]
    return vals.transpose(0, 1, 3, 2).reshape(g * 512, n)


B, N, T, D, NQ = 1, 512, 2048, 512, 256


def setup_inputs():
    n = np.random.standard_normal
    idx = np.random.permutation(T)[:B * N]
    idx2 = np.random.permutation(1024)[:B * N]
    s = mx_kscale(D)[:, None]
    kp = pack_weight(n((D, T)) / s, "e4m3")
    return {
        "qT": (n((B, D, NQ)) * s * (1.00 / np.sqrt(D))).astype(np.float32),
        "k_words": kp[0],
        "k_scales": kp[1],
        "cT": (n((D, 1024)) / s).astype(np.float32),
        "offs": striped(idx),
        "offs2": striped(idx2),
    }


def reference(qT, k_words, k_scales, cT, offs, offs2):
    idx = unstriped(offs)
    idx2 = unstriped(offs2)
    pick = lambda x, which: x[:, which].reshape(x.shape[0], B, -1).transpose(1, 0, 2)
    k = unpack_weight(k_words, k_scales, "e4m3")
    kg = pick(k, idx)
    cg = mxq(pick(f64(cT), idx2), 1, "e4m3")
    qq = mxq(f64(qT), 1, "e4m3")
    a = qq.transpose(0, 2, 1) @ kg
    z = qq.transpose(0, 2, 1) @ cg
    m = np.maximum(np.max(a, axis=-1, keepdims=True), np.max(z, axis=-1, keepdims=True))
    e = np.exp(z - m)
    l = np.sum(e, axis=-1, keepdims=True) + np.sum(np.exp(a - m), axis=-1, keepdims=True)
    y = e / l
    return y

@@ -1,0 +1,149 @@
+from contextlib import ExitStack
+
+import concourse.mybir as mybir
+
+D, NQ, N, T, TC = 512, 256, 512, 2048, 1024
+FLOPS = 2 * 2 * D * NQ * N
+
+F32 = mybir.dt.float32
+BF16 = mybir.dt.bfloat16
+I32 = mybir.dt.int32
+U32 = mybir.dt.uint32
+U16 = mybir.dt.uint16
+U8 = mybir.dt.uint8
+FP8X4 = mybir.dt.float8_e4m3fn_x4
+ALU = mybir.AluOpType
+ACT = mybir.ActivationFunctionType
+
+P = 128
+PACK = 4
+CHUNK = 512
+LAST_ON_VECTOR = 320
+
+
+def tile_attend_locmix_topk_kernel(tc, qT, k_words, k_scales, cT, offs, offs2, out):
+    nc = tc.nc
+    with ExitStack() as ctx:
+        lists = ctx.enter_context(tc.tile_pool(name="lists", bufs=1))
+        sb = ctx.enter_context(tc.tile_pool(name="sb", bufs=1))
+        psum = ctx.enter_context(tc.psum_pool(name="psum", bufs=1))
+
+        warm = sb.tile([P, 1], F32, name="warm")
+        warm_out = sb.tile([P, 1], F32, name="warm_out")
+        nc.vector.memset(warm[:], 0.0)
+        nc.scalar.activation(warm_out[:], warm[:], ACT.Exp)
+
+        scale_pool = sb.tile([P, T // 4], I32, name="scale_pool", align_bytes=64)
+        nc.vector.memset(scale_pool[:], 0)
+
+        c_list = lists.tile([P, N // 16], U16, name="c_list")
+        k_list = lists.tile([P, N // 16], U16, name="k_list")
+        nc.sync.dma_start(k_list[:], offs)
+        nc.sync.dma_start(c_list[:], offs2)
+
+        scale_rows = k_scales[0].bitcast(I32)
+        for quad in range(4):
+            nc.scalar.dma_start(scale_pool[32 * quad : 32 * quad + 4, :], scale_rows[4 * quad : 4 * quad + 4, :])
+
+        c_rows = cT.rearrange("(p t) n -> p t n", t=PACK)
+        c_raw = {}
+        for u in range(2):
+            for h in range(TC // CHUNK):
+                c_raw[u, h] = sb.tile([P, 2, CHUNK], F32, name="c_raw%d%d" % (u, h))
+                nc.sync.dma_start(c_raw[u, h][:], c_rows[:, 2 * u : 2 * u + 2, h * CHUNK : (h + 1) * CHUNK])
+        q_raw = sb.tile([P, PACK, NQ], F32, name="q_raw")
+        nc.sync.dma_start(q_raw[:], qT[0].rearrange("(p t) n -> p t n", t=PACK))
+        k_pool = sb.tile([P, T], I32, name="k_pool", align_bytes=64)
+        nc.sync.dma_start(k_pool[:], k_words[0].rearrange("p n r -> p (n r)").bitcast(I32))
+
+        k_scale = sb.tile([P, N], U8, name="k_scale", align_bytes=64)
+        nc.vector.tensor_copy(k_scale[:], scale_pool[:].bitcast(U8).indirect(k_list[:]))
+
+        c_pairs = sb.tile([P, 2, N], U32, name="c_pairs", align_bytes=64)
+        for u in range(2):
+            pair_pool = sb.tile([P, TC, 2], BF16, name="pair_pool%d" % u, align_bytes=64)
+            for h in range(TC // CHUNK):
+                src = c_raw[u, h][:].rearrange("p e n -> p n e")
+                dst = pair_pool[:, h * CHUNK : (h + 1) * CHUNK, :]
+                if (u, h) == (1, 1):
+                    nc.vector.tensor_copy(dst[:, :LAST_ON_VECTOR, :], src[:, :LAST_ON_VECTOR, :])
+                    nc.scalar.copy(dst[:, LAST_ON_VECTOR:, :], src[:, LAST_ON_VECTOR:, :])
+                else:
+                    nc.scalar.copy(dst, src)
+            window = pair_pool[:].rearrange("p n e -> p (n e)").bitcast(U32)
+            nc.vector.tensor_copy(c_pairs[:, u, :], window.indirect(c_list[:]))
+
+        q_bf = sb.tile([P, NQ, PACK], BF16, name="q_bf", align_bytes=64)
+        nc.scalar.copy(q_bf[:], q_raw[:].rearrange("p t n -> p n t"))
+
+        c_bf = sb.tile([P, N, 2, 2], BF16, name="c_bf", align_bytes=64)
+        pairs_bf = c_pairs[:].rearrange("p u n -> p (u n)").bitcast(BF16).rearrange("p (u n e) -> p n u e", u=2, e=2)
+        c_code = sb.tile([P, N], U32, name="c_code", align_bytes=64)
+        c_scale = sb.tile([P, N], U8, name="c_scale", align_bytes=64)
+        half = N // 2
+        for h in range(2):
+            nc.vector.tensor_copy(c_bf[:, h * half : (h + 1) * half], pairs_bf[:, h * half : (h + 1) * half])
+        for h in range(2):
+            cols = slice(h * half, (h + 1) * half)
+            nc.vector.quantize_mx(
+                out=c_code[:, cols].bitcast(FP8X4),
+                scales=c_scale[:, cols],
+                in_=c_bf[:, cols].rearrange("p n u e -> p (n u e)"),
+            )
+        q_code = sb.tile([P, NQ], U32, name="q_code", align_bytes=64)
+        q_scale = sb.tile([P, NQ], U8, name="q_scale", align_bytes=64)
+        nc.vector.quantize_mx(
+            out=q_code[:].bitcast(FP8X4), scales=q_scale[:], in_=q_bf[:].rearrange("p n t -> p (n t)")
+        )
+
+        def scores(name, b, code, scale):
+            bank = psum.tile([P, N], F32, name=name)
+            rows = slice(b * P, (b + 1) * P)
+            nc.tensor.matmul_mx(
+                out=bank[:],
+                lhsT=q_code[:, rows].bitcast(FP8X4),
+                lhsT_scale=q_scale[:, rows],
+                rhs=code[:].bitcast(FP8X4),
+                rhs_scale=scale[:],
+                start=True,
+                stop=True,
+            )
+            return bank
+
+        z_bank = [scores("z%d" % b, b, c_code, c_scale) for b in range(2)]
+
+        k_code = sb.tile([P, N], U32, name="k_code", align_bytes=64)
+        nc.vector.tensor_copy(k_code[:], k_pool[:].bitcast(U32).indirect(k_list[:]))
+        a_bank = [scores("a%d" % b, b, k_code, k_scale) for b in range(2)]
+
+        def col(name):
+            return sb.tile([P, 1], F32, name=name)
+
+        neg_mz, e_z, l_z = [], [], []
+        for b in range(2):
+            neg_z = sb.tile([P, N], F32, name="neg_z%d" % b)
+            neg_mz.append(col("neg_mz%d" % b))
+            nc.vector.tensor_scalar(neg_z[:], z_bank[b][:], -1.0, None, ALU.mult, ALU.min, accum_out=neg_mz[b][:])
+            e_z.append(sb.tile([P, N], F32, name="e_z%d" % b))
+            l_z.append(col("l_z%d" % b))
+            nc.scalar.activation(e_z[b][:], neg_z[:], ACT.Exp, bias=neg_mz[b][:], scale=-1.0, accum_out=l_z[b][:])
+
+        shift, l_a = [], []
+        for b in range(2):
+            neg_a = sb.tile([P, N], F32, name="neg_a%d" % b)
+            neg_m = col("neg_m%d" % b)
+            nc.vector.tensor_scalar(neg_a[:], a_bank[b][:], -1.0, neg_mz[b][:], ALU.mult, ALU.min, accum_out=neg_m[:])
+            shift.append(col("shift%d" % b))
+            nc.scalar.activation(shift[b][:], neg_mz[b][:], ACT.Exp, bias=neg_m[:], scale=-1.0)
+            e_a = sb.tile([P, N], F32, name="e_a%d" % b)
+            l_a.append(col("l_a%d" % b))
+            nc.scalar.activation(e_a[:], neg_a[:], ACT.Exp, bias=neg_m[:], scale=-1.0, accum_out=l_a[b][:])
+
+        for b in range(2):
+            total = col("total%d" % b)
+            nc.vector.tensor_scalar(total[:], l_z[b][:], shift[b][:], l_a[b][:], ALU.mult, ALU.add)
+            inv = col("inv%d" % b)
+            nc.vector.reciprocal(inv[:], total[:])
+            y = sb.tile([P, N], F32, name="y%d" % b)
+            nc.vector.tensor_scalar(y[:], e_z[b][:], shift[b][:], inv[:], ALU.mult, ALU.mult)
+            nc.sync.dma_start(out[0, b * P : (b + 1) * P, :], y[:])

@@ -28,32 +28,34 @@ def tile_attend_locmix_topk_kernel(tc, qT, k_words, k_scales, cT, offs, offs2, o
         sb = ctx.enter_context(tc.tile_pool(name="sb", bufs=1))
         psum = ctx.enter_context(tc.psum_pool(name="psum", bufs=1))
 
+        scale_pool = sb.tile([P, T // 4], I32, name="scale_pool", align_bytes=64)
+        nc.vector.memset(scale_pool[:], 0)
+
         warm = sb.tile([P, 1], F32, name="warm")
         warm_out = sb.tile([P, 1], F32, name="warm_out")
         nc.vector.memset(warm[:], 0.0)
         nc.scalar.activation(warm_out[:], warm[:], ACT.Exp)
 
-        scale_pool = sb.tile([P, T // 4], I32, name="scale_pool", align_bytes=64)
-        nc.vector.memset(scale_pool[:], 0)
-
         c_list = lists.tile([P, N // 16], U16, name="c_list")
         k_list = lists.tile([P, N // 16], U16, name="k_list")
         nc.sync.dma_start(k_list[:], offs)
-        nc.sync.dma_start(c_list[:], offs2)
-
-        scale_rows = k_scales[0].bitcast(I32)
-        for quad in range(4):
-            nc.scalar.dma_start(scale_pool[32 * quad : 32 * quad + 4, :], scale_rows[4 * quad : 4 * quad + 4, :])
 
         c_rows = cT.rearrange("(p t) n -> p t n", t=PACK)
+        scale_rows = k_scales[0].bitcast(I32)
         c_raw = {}
         for u in range(2):
             for h in range(TC // CHUNK):
                 c_raw[u, h] = sb.tile([P, 2, CHUNK], F32, name="c_raw%d%d" % (u, h))
                 nc.sync.dma_start(c_raw[u, h][:], c_rows[:, 2 * u : 2 * u + 2, h * CHUNK : (h + 1) * CHUNK])
+                if (u, h) == (0, 0):
+                    for quad in range(4):
+                        nc.sync.dma_start(
+                            scale_pool[32 * quad : 32 * quad + 4, :], scale_rows[4 * quad : 4 * quad + 4, :]
+                        )
+                    nc.sync.dma_start(c_list[:], offs2)
         q_raw = sb.tile([P, PACK, NQ], F32, name="q_raw")
         nc.sync.dma_start(q_raw[:], qT[0].rearrange("(p t) n -> p t n", t=PACK))
-        k_pool = sb.tile([P, T], I32, name="k_pool", align_bytes=64)
+        k_pool = sb.tile([P, T], I32, name="k_pool", tag="k_then_neg", align_bytes=64)
         nc.sync.dma_start(k_pool[:], k_words[0].rearrange("p n r -> p (n r)").bitcast(I32))
 
         k_scale = sb.tile([P, N], U8, name="k_scale", align_bytes=64)
@@ -71,18 +73,30 @@ def tile_attend_locmix_topk_kernel(tc, qT, k_words, k_scales, cT, offs, offs2, o
                 else:
                     nc.scalar.copy(dst, src)
             window = pair_pool[:].rearrange("p n e -> p (n e)").bitcast(U32)
-            nc.vector.tensor_copy(c_pairs[:, u, :], window.indirect(c_list[:]))
+            if u == 0:
+                nc.vector.tensor_copy(c_pairs[:, u, :], window.indirect(c_list[:]))
+            else:
+                for h in range(2):
+                    nc.vector.tensor_copy(
+                        c_pairs[:, u, h * 256 : (h + 1) * 256], window.indirect(c_list[:, h * 16 : (h + 1) * 16])
+                    )
 
         q_bf = sb.tile([P, NQ, PACK], BF16, name="q_bf", align_bytes=64)
         nc.scalar.copy(q_bf[:], q_raw[:].rearrange("p t n -> p n t"))
 
         c_bf = sb.tile([P, N, 2, 2], BF16, name="c_bf", align_bytes=64)
-        pairs_bf = c_pairs[:].rearrange("p u n -> p (u n)").bitcast(BF16).rearrange("p (u n e) -> p n u e", u=2, e=2)
+        c_words = c_bf[:].rearrange("p n u e -> p (n u e)").bitcast(I32).rearrange("p (n u) -> p n u", u=2)
+        pair_words = c_pairs[:].bitcast(I32).rearrange("p u n -> p n u")
         c_code = sb.tile([P, N], U32, name="c_code", align_bytes=64)
         c_scale = sb.tile([P, N], U8, name="c_scale", align_bytes=64)
         half = N // 2
         for h in range(2):
-            nc.vector.tensor_copy(c_bf[:, h * half : (h + 1) * half], pairs_bf[:, h * half : (h + 1) * half])
+            nc.vector.tensor_copy(c_words[:, h * half : (h + 1) * half], pair_words[:, h * half : (h + 1) * half])
+        q_code = sb.tile([P, NQ], U32, name="q_code", align_bytes=64)
+        q_scale = sb.tile([P, NQ], U8, name="q_scale", align_bytes=64)
+        nc.vector.quantize_mx(
+            out=q_code[:].bitcast(FP8X4), scales=q_scale[:], in_=q_bf[:].rearrange("p n t -> p (n t)")
+        )
         for h in range(2):
             cols = slice(h * half, (h + 1) * half)
             nc.vector.quantize_mx(
@@ -90,60 +104,60 @@ def tile_attend_locmix_topk_kernel(tc, qT, k_words, k_scales, cT, offs, offs2, o
                 scales=c_scale[:, cols],
                 in_=c_bf[:, cols].rearrange("p n u e -> p (n u e)"),
             )
-        q_code = sb.tile([P, NQ], U32, name="q_code", align_bytes=64)
-        q_scale = sb.tile([P, NQ], U8, name="q_scale", align_bytes=64)
-        nc.vector.quantize_mx(
-            out=q_code[:].bitcast(FP8X4), scales=q_scale[:], in_=q_bf[:].rearrange("p n t -> p (n t)")
-        )
-
-        def scores(name, b, code, scale):
-            bank = psum.tile([P, N], F32, name=name)
+        def scores(bank, b, h, code, scale):
             rows = slice(b * P, (b + 1) * P)
+            cols = slice(h * half, (h + 1) * half)
             nc.tensor.matmul_mx(
-                out=bank[:],
+                out=bank[:, cols],
                 lhsT=q_code[:, rows].bitcast(FP8X4),
                 lhsT_scale=q_scale[:, rows],
-                rhs=code[:].bitcast(FP8X4),
-                rhs_scale=scale[:],
+                rhs=code[:, cols].bitcast(FP8X4),
+                rhs_scale=scale[:, cols],
                 start=True,
                 stop=True,
             )
-            return bank
 
-        z_bank = [scores("z%d" % b, b, c_code, c_scale) for b in range(2)]
+        z_bank = [psum.tile([P, N], F32, name="z%d" % b) for b in range(2)]
+        a_bank = [psum.tile([P, N], F32, name="a%d" % b) for b in range(2)]
+        for b in range(2):
+            for h in range(2):
+                scores(z_bank[b], b, h, c_code, c_scale)
 
         k_code = sb.tile([P, N], U32, name="k_code", align_bytes=64)
-        nc.vector.tensor_copy(k_code[:], k_pool[:].bitcast(U32).indirect(k_list[:]))
-        a_bank = [scores("a%d" % b, b, k_code, k_scale) for b in range(2)]
+        for h in range(2):
+            nc.vector.tensor_copy(
+                k_code[:, h * half : (h + 1) * half], k_pool[:].bitcast(U32).indirect(k_list[:, h * 16 : (h + 1) * 16])
+            )
+        for h in range(2):
+            for b in range(2):
+                scores(a_bank[b], b, h, k_code, k_scale)
 
         def col(name):
             return sb.tile([P, 1], F32, name=name)
 
-        neg_mz, e_z, l_z = [], [], []
+        neg_both = sb.tile([P, 2, 1024], F32, name="neg_both", tag="k_then_neg", align_bytes=64)
+        e_z, l_z1, e_a, l_a = [], [], [], []
         for b in range(2):
-            neg_z = sb.tile([P, N], F32, name="neg_z%d" % b)
-            neg_mz.append(col("neg_mz%d" % b))
-            nc.vector.tensor_scalar(neg_z[:], z_bank[b][:], -1.0, None, ALU.mult, ALU.min, accum_out=neg_mz[b][:])
+            neg_a = neg_both[:, b, : N + 1]
+            neg_mz = neg_both[:, b, N : N + 1]
+            nc.vector.tensor_reduce(neg_mz, z_bank[b][:], mybir.AxisListType.X, ALU.max, negate=True)
             e_z.append(sb.tile([P, N], F32, name="e_z%d" % b))
-            l_z.append(col("l_z%d" % b))
-            nc.scalar.activation(e_z[b][:], neg_z[:], ACT.Exp, bias=neg_mz[b][:], scale=-1.0, accum_out=l_z[b][:])
-
-        shift, l_a = [], []
-        for b in range(2):
-            neg_a = sb.tile([P, N], F32, name="neg_a%d" % b)
+            l_z = col("l_z%d" % b)
+            nc.scalar.activation(e_z[b][:], z_bank[b][:], ACT.Exp, bias=neg_mz, accum_out=l_z[:])
+            l_z1.append(col("l_z1%d" % b))
+            nc.gpsimd.tensor_scalar(l_z1[b][:], l_z[:], -1.0, 1.0, ALU.add, ALU.mult)
             neg_m = col("neg_m%d" % b)
-            nc.vector.tensor_scalar(neg_a[:], a_bank[b][:], -1.0, neg_mz[b][:], ALU.mult, ALU.min, accum_out=neg_m[:])
-            shift.append(col("shift%d" % b))
-            nc.scalar.activation(shift[b][:], neg_mz[b][:], ACT.Exp, bias=neg_m[:], scale=-1.0)
-            e_a = sb.tile([P, N], F32, name="e_a%d" % b)
+            nc.vector.tensor_scalar(neg_a[:, :N], a_bank[b][:], -1.0, neg_mz, ALU.mult, ALU.min, accum_out=neg_m[:])
+            e_a.append(sb.tile([P, N + 1], F32, name="e_a%d" % b))
             l_a.append(col("l_a%d" % b))
-            nc.scalar.activation(e_a[:], neg_a[:], ACT.Exp, bias=neg_m[:], scale=-1.0, accum_out=l_a[b][:])
+            nc.scalar.activation(e_a[b][:], neg_a, ACT.Exp, bias=neg_m[:], scale=-1.0, accum_out=l_a[b][:])
 
         for b in range(2):
+            shift = e_a[b][:, N : N + 1]
             total = col("total%d" % b)
-            nc.vector.tensor_scalar(total[:], l_z[b][:], shift[b][:], l_a[b][:], ALU.mult, ALU.add)
+            nc.vector.tensor_scalar(total[:], l_z1[b][:], shift, l_a[b][:], ALU.mult, ALU.add)
             inv = col("inv%d" % b)
             nc.vector.reciprocal(inv[:], total[:])
             y = sb.tile([P, N], F32, name="y%d" % b)
-            nc.vector.tensor_scalar(y[:], e_z[b][:], shift[b][:], inv[:], ALU.mult, ALU.mult)
+            nc.vector.tensor_scalar(y[:], e_z[b][:], shift, inv[:], ALU.mult, ALU.mult)
             nc.sync.dma_start(out[0, b * P : (b + 1) * P, :], y[:])

@@ -61,37 +61,33 @@ def tile_attend_locmix_topk_kernel(tc, qT, k_words, k_scales, cT, offs, offs2, o
         k_scale = sb.tile([P, N], U8, name="k_scale", align_bytes=64)
         nc.vector.tensor_copy(k_scale[:], scale_pool[:].bitcast(U8).indirect(k_list[:]))
 
-        c_pairs = sb.tile([P, 2, N], U32, name="c_pairs", align_bytes=64)
+        c_bf = sb.tile([P, N, 2, 2], BF16, name="c_bf", align_bytes=64)
+        c_words = c_bf[:].rearrange("p n u e -> p (n u e)").bitcast(U32).rearrange("p (n u) -> p n u", u=2)
         for u in range(2):
             pair_pool = sb.tile([P, TC, 2], BF16, name="pair_pool%d" % u, align_bytes=64)
             for h in range(TC // CHUNK):
                 src = c_raw[u, h][:].rearrange("p e n -> p n e")
                 dst = pair_pool[:, h * CHUNK : (h + 1) * CHUNK, :]
-                if (u, h) == (1, 1):
+                if h == 1:
                     nc.vector.tensor_copy(dst[:, :LAST_ON_VECTOR, :], src[:, :LAST_ON_VECTOR, :])
                     nc.scalar.copy(dst[:, LAST_ON_VECTOR:, :], src[:, LAST_ON_VECTOR:, :])
                 else:
                     nc.scalar.copy(dst, src)
             window = pair_pool[:].rearrange("p n e -> p (n e)").bitcast(U32)
             if u == 0:
-                nc.vector.tensor_copy(c_pairs[:, u, :], window.indirect(c_list[:]))
+                nc.vector.tensor_copy(c_words[:, :, u], window.indirect(c_list[:]))
             else:
                 for h in range(2):
                     nc.vector.tensor_copy(
-                        c_pairs[:, u, h * 256 : (h + 1) * 256], window.indirect(c_list[:, h * 16 : (h + 1) * 16])
+                        c_words[:, h * 256 : (h + 1) * 256, u], window.indirect(c_list[:, h * 16 : (h + 1) * 16])
                     )
 
         q_bf = sb.tile([P, NQ, PACK], BF16, name="q_bf", align_bytes=64)
         nc.scalar.copy(q_bf[:], q_raw[:].rearrange("p t n -> p n t"))
 
-        c_bf = sb.tile([P, N, 2, 2], BF16, name="c_bf", align_bytes=64)
-        c_words = c_bf[:].rearrange("p n u e -> p (n u e)").bitcast(I32).rearrange("p (n u) -> p n u", u=2)
-        pair_words = c_pairs[:].bitcast(I32).rearrange("p u n -> p n u")
         c_code = sb.tile([P, N], U32, name="c_code", align_bytes=64)
         c_scale = sb.tile([P, N], U8, name="c_scale", align_bytes=64)
         half = N // 2
-        for h in range(2):
-            nc.vector.tensor_copy(c_words[:, h * half : (h + 1) * half], pair_words[:, h * half : (h + 1) * half])
         q_code = sb.tile([P, NQ], U32, name="q_code", align_bytes=64)
         q_scale = sb.tile([P, NQ], U8, name="q_scale", align_bytes=64)
         nc.vector.quantize_mx(
@@ -138,26 +134,40 @@ def tile_attend_locmix_topk_kernel(tc, qT, k_words, k_scales, cT, offs, offs2, o
         neg_both = sb.tile([P, 2, 1024], F32, name="neg_both", tag="k_then_neg", align_bytes=64)
         e_z, l_z1, e_a, l_a = [], [], [], []
         for b in range(2):
-            neg_a = neg_both[:, b, : N + 1]
             neg_mz = neg_both[:, b, N : N + 1]
             nc.vector.tensor_reduce(neg_mz, z_bank[b][:], mybir.AxisListType.X, ALU.max, negate=True)
             e_z.append(sb.tile([P, N], F32, name="e_z%d" % b))
             l_z = col("l_z%d" % b)
             nc.scalar.activation(e_z[b][:], z_bank[b][:], ACT.Exp, bias=neg_mz, accum_out=l_z[:])
             l_z1.append(col("l_z1%d" % b))
-            nc.gpsimd.tensor_scalar(l_z1[b][:], l_z[:], -1.0, 1.0, ALU.add, ALU.mult)
+            nc.scalar.activation(l_z1[b][:], l_z[:], ACT.Identity, bias=-1.0)
+        for b in range(2):
+            neg_a = neg_both[:, b, : N + 1]
+            neg_mz = neg_both[:, b, N : N + 1]
             neg_m = col("neg_m%d" % b)
             nc.vector.tensor_scalar(neg_a[:, :N], a_bank[b][:], -1.0, neg_mz, ALU.mult, ALU.min, accum_out=neg_m[:])
             e_a.append(sb.tile([P, N + 1], F32, name="e_a%d" % b))
             l_a.append(col("l_a%d" % b))
             nc.scalar.activation(e_a[b][:], neg_a, ACT.Exp, bias=neg_m[:], scale=-1.0, accum_out=l_a[b][:])
 
-        for b in range(2):
-            shift = e_a[b][:, N : N + 1]
-            total = col("total%d" % b)
-            nc.vector.tensor_scalar(total[:], l_z1[b][:], shift, l_a[b][:], ALU.mult, ALU.add)
-            inv = col("inv%d" % b)
-            nc.vector.reciprocal(inv[:], total[:])
-            y = sb.tile([P, N], F32, name="y%d" % b)
-            nc.vector.tensor_scalar(y[:], e_z[b][:], shift, inv[:], ALU.mult, ALU.mult)
-            nc.sync.dma_start(out[0, b * P : (b + 1) * P, :], y[:])
+        shift = [e_a[b][:, N : N + 1] for b in range(2)]
+        total = [col("total%d" % b) for b in range(2)]
+        inv = [col("inv%d" % b) for b in range(2)]
+        y = [
+            sb.tile([P, N], F32, name="y0", tag="k_then_neg", align_bytes=64),
+            sb.tile([P, N], F32, name="y1"),
+        ]
+
+        def row_sum(b):
+            nc.vector.tensor_scalar(total[b][:], l_z1[b][:], shift[b], l_a[b][:], ALU.mult, ALU.add)
+
+        def weights(b):
+            nc.vector.tensor_scalar(y[b][:], e_z[b][:], shift[b], inv[b][:], ALU.mult, ALU.mult)
+            nc.sync.dma_start(out[0, b * P : (b + 1) * P, :], y[b][:])
+
+        row_sum(0)
+        nc.vector.reciprocal(inv[0][:], total[0][:])
+        row_sum(1)
+        weights(0)
+        nc.vector.reciprocal(inv[1][:], total[1][:])
+        weights(1)

@@ -18,7 +18,7 @@ ACT = mybir.ActivationFunctionType
 P = 128
 PACK = 4
 CHUNK = 512
-LAST_ON_VECTOR = 320
+LAST_ON_VECTOR = 256
 
 
 def tile_attend_locmix_topk_kernel(tc, qT, k_words, k_scales, cT, offs, offs2, out):
@@ -53,7 +53,7 @@ def tile_attend_locmix_topk_kernel(tc, qT, k_words, k_scales, cT, offs, offs2, o
                             scale_pool[32 * quad : 32 * quad + 4, :], scale_rows[4 * quad : 4 * quad + 4, :]
                         )
                     nc.sync.dma_start(c_list[:], offs2)
-        q_raw = sb.tile([P, PACK, NQ], F32, name="q_raw")
+        q_raw = sb.tile([P, PACK, NQ], F32, name="q_raw", tag="q_then_c", align_bytes=64)
         nc.sync.dma_start(q_raw[:], qT[0].rearrange("(p t) n -> p t n", t=PACK))
         k_pool = sb.tile([P, T], I32, name="k_pool", tag="k_then_neg", align_bytes=64)
         nc.sync.dma_start(k_pool[:], k_words[0].rearrange("p n r -> p (n r)").bitcast(I32))
@@ -61,8 +61,7 @@ def tile_attend_locmix_topk_kernel(tc, qT, k_words, k_scales, cT, offs, offs2, o
         k_scale = sb.tile([P, N], U8, name="k_scale", align_bytes=64)
         nc.vector.tensor_copy(k_scale[:], scale_pool[:].bitcast(U8).indirect(k_list[:]))
 
-        c_bf = sb.tile([P, N, 2, 2], BF16, name="c_bf", align_bytes=64)
-        c_words = c_bf[:].rearrange("p n u e -> p (n u e)").bitcast(U32).rearrange("p (n u) -> p n u", u=2)
+        c_pairs = sb.tile([P, 2, N], U32, name="c_pairs", align_bytes=64)
         for u in range(2):
             pair_pool = sb.tile([P, TC, 2], BF16, name="pair_pool%d" % u, align_bytes=64)
             for h in range(TC // CHUNK):
@@ -75,30 +74,42 @@ def tile_attend_locmix_topk_kernel(tc, qT, k_words, k_scales, cT, offs, offs2, o
                     nc.scalar.copy(dst, src)
             window = pair_pool[:].rearrange("p n e -> p (n e)").bitcast(U32)
             if u == 0:
-                nc.vector.tensor_copy(c_words[:, :, u], window.indirect(c_list[:]))
+                nc.vector.tensor_copy(c_pairs[:, u, :], window.indirect(c_list[:]))
             else:
                 for h in range(2):
                     nc.vector.tensor_copy(
-                        c_words[:, h * 256 : (h + 1) * 256, u], window.indirect(c_list[:, h * 16 : (h + 1) * 16])
+                        c_pairs[:, u, h * 256 : (h + 1) * 256], window.indirect(c_list[:, h * 16 : (h + 1) * 16])
                     )
 
-        q_bf = sb.tile([P, NQ, PACK], BF16, name="q_bf", align_bytes=64)
-        nc.scalar.copy(q_bf[:], q_raw[:].rearrange("p t n -> p n t"))
+        q_bf = sb.tile([P, NQ, PACK], BF16, name="q_bf", tag="q_then_codes", align_bytes=64)
+        nc.scalar.copy(
+            q_bf[:].rearrange("p (c i) t -> p c t i", i=4), q_raw[:].rearrange("p t (c i) -> p c t i", i=4)
+        )
 
-        c_code = sb.tile([P, N], U32, name="c_code", align_bytes=64)
         c_scale = sb.tile([P, N], U8, name="c_scale", align_bytes=64)
         half = N // 2
+        c_bf = [
+            sb.tile([P, half * PACK], BF16, name="c_bf0", align_bytes=64),
+            sb.tile([P, half * PACK], BF16, name="c_bf1", tag="q_then_c", align_bytes=64),
+        ]
+        for h, engine_copy, word in ((0, nc.vector.tensor_copy, I32), (1, nc.scalar.copy, F32)):
+            cols = slice(h * half, (h + 1) * half)
+            engine_copy(
+                c_bf[h][:].bitcast(word).rearrange("p (n u) -> p n u", u=2),
+                c_pairs[:].bitcast(word).rearrange("p u n -> p n u")[:, cols],
+            )
         q_code = sb.tile([P, NQ], U32, name="q_code", align_bytes=64)
         q_scale = sb.tile([P, NQ], U8, name="q_scale", align_bytes=64)
         nc.vector.quantize_mx(
             out=q_code[:].bitcast(FP8X4), scales=q_scale[:], in_=q_bf[:].rearrange("p n t -> p (n t)")
         )
+        c_code = sb.tile([P, N], U32, name="c_code", tag="q_then_codes", align_bytes=64)
         for h in range(2):
             cols = slice(h * half, (h + 1) * half)
             nc.vector.quantize_mx(
                 out=c_code[:, cols].bitcast(FP8X4),
                 scales=c_scale[:, cols],
-                in_=c_bf[:, cols].rearrange("p n u e -> p (n u e)"),
+                in_=c_bf[h][:],
             )
         def scores(bank, b, h, code, scale):
             rows = slice(b * P, (b + 1) * P)
@@ -132,15 +143,15 @@ def tile_attend_locmix_topk_kernel(tc, qT, k_words, k_scales, cT, offs, offs2, o
             return sb.tile([P, 1], F32, name=name)
 
         neg_both = sb.tile([P, 2, 1024], F32, name="neg_both", tag="k_then_neg", align_bytes=64)
-        e_z, l_z1, e_a, l_a = [], [], [], []
+        e_z, e_a, l_a = [], [], []
+        l_z = sb.tile([P, 2], F32, name="l_z")
+        l_z1 = sb.tile([P, 2], F32, name="l_z1")
         for b in range(2):
             neg_mz = neg_both[:, b, N : N + 1]
             nc.vector.tensor_reduce(neg_mz, z_bank[b][:], mybir.AxisListType.X, ALU.max, negate=True)
             e_z.append(sb.tile([P, N], F32, name="e_z%d" % b))
-            l_z = col("l_z%d" % b)
-            nc.scalar.activation(e_z[b][:], z_bank[b][:], ACT.Exp, bias=neg_mz, accum_out=l_z[:])
-            l_z1.append(col("l_z1%d" % b))
-            nc.scalar.activation(l_z1[b][:], l_z[:], ACT.Identity, bias=-1.0)
+            nc.scalar.activation(e_z[b][:], z_bank[b][:], ACT.Exp, bias=neg_mz, accum_out=l_z[:, b : b + 1])
+            nc.scalar.activation(l_z1[:, b : b + 1], l_z[:, b : b + 1], ACT.Identity, bias=-1.0)
         for b in range(2):
             neg_a = neg_both[:, b, : N + 1]
             neg_mz = neg_both[:, b, N : N + 1]
@@ -159,7 +170,7 @@ def tile_attend_locmix_topk_kernel(tc, qT, k_words, k_scales, cT, offs, offs2, o
         ]
 
         def row_sum(b):
-            nc.vector.tensor_scalar(total[b][:], l_z1[b][:], shift[b], l_a[b][:], ALU.mult, ALU.add)
+            nc.vector.tensor_scalar(total[b][:], l_z1[:, b : b + 1], shift[b], l_a[b][:], ALU.mult, ALU.add)
 
         def weights(b):
             nc.vector.tensor_scalar(y[b][:], e_z[b][:], shift[b], inv[b][:], ALU.mult, ALU.mult)

@@ -142,19 +142,22 @@ def tile_attend_locmix_topk_kernel(tc, qT, k_words, k_scales, cT, offs, offs2, o
         def col(name):
             return sb.tile([P, 1], F32, name=name)
 
-        neg_both = sb.tile([P, 2, 1024], F32, name="neg_both", tag="k_then_neg", align_bytes=64)
+        neg = [
+            sb.tile([P, N + 1], F32, name="neg0"),
+            sb.tile([P, N + 1], F32, name="neg1", tag="k_then_neg", align_bytes=64),
+        ]
         e_z, e_a, l_a = [], [], []
         l_z = sb.tile([P, 2], F32, name="l_z")
         l_z1 = sb.tile([P, 2], F32, name="l_z1")
         for b in range(2):
-            neg_mz = neg_both[:, b, N : N + 1]
+            neg_mz = neg[b][:, N : N + 1]
             nc.vector.tensor_reduce(neg_mz, z_bank[b][:], mybir.AxisListType.X, ALU.max, negate=True)
             e_z.append(sb.tile([P, N], F32, name="e_z%d" % b))
             nc.scalar.activation(e_z[b][:], z_bank[b][:], ACT.Exp, bias=neg_mz, accum_out=l_z[:, b : b + 1])
             nc.scalar.activation(l_z1[:, b : b + 1], l_z[:, b : b + 1], ACT.Identity, bias=-1.0)
         for b in range(2):
-            neg_a = neg_both[:, b, : N + 1]
-            neg_mz = neg_both[:, b, N : N + 1]
+            neg_a = neg[b][:]
+            neg_mz = neg[b][:, N : N + 1]
             neg_m = col("neg_m%d" % b)
             nc.vector.tensor_scalar(neg_a[:, :N], a_bank[b][:], -1.0, neg_mz, ALU.mult, ALU.min, accum_out=neg_m[:])
             e_a.append(sb.tile([P, N + 1], F32, name="e_a%d" % b))

@@ -17,8 +17,7 @@ ACT = mybir.ActivationFunctionType
 
 P = 128
 PACK = 4
-CHUNK = 512
-LAST_ON_VECTOR = 256
+HALF = N // 2
 
 
 def tile_attend_locmix_topk_kernel(tc, qT, k_words, k_scales, cT, offs, offs2, out):
@@ -26,11 +25,11 @@ def tile_attend_locmix_topk_kernel(tc, qT, k_words, k_scales, cT, offs, offs2, o
     with ExitStack() as ctx:
         lists = ctx.enter_context(tc.tile_pool(name="lists", bufs=1))
         sb = ctx.enter_context(tc.tile_pool(name="sb", bufs=1))
+        late = ctx.enter_context(tc.tile_pool(name="late", bufs=1))
         psum = ctx.enter_context(tc.psum_pool(name="psum", bufs=1))
 
         scale_pool = sb.tile([P, T // 4], I32, name="scale_pool", align_bytes=64)
         nc.vector.memset(scale_pool[:], 0)
-
         warm = sb.tile([P, 1], F32, name="warm")
         warm_out = sb.tile([P, 1], F32, name="warm_out")
         nc.vector.memset(warm[:], 0.0)
@@ -38,86 +37,83 @@ def tile_attend_locmix_topk_kernel(tc, qT, k_words, k_scales, cT, offs, offs2, o
 
         c_list = lists.tile([P, N // 16], U16, name="c_list")
         k_list = lists.tile([P, N // 16], U16, name="k_list")
-        nc.sync.dma_start(k_list[:], offs)
-
         c_rows = cT.rearrange("(p t) n -> p t n", t=PACK)
         scale_rows = k_scales[0].bitcast(I32)
-        c_raw = {}
-        for u in range(2):
-            for h in range(TC // CHUNK):
-                c_raw[u, h] = sb.tile([P, 2, CHUNK], F32, name="c_raw%d%d" % (u, h))
-                nc.sync.dma_start(c_raw[u, h][:], c_rows[:, 2 * u : 2 * u + 2, h * CHUNK : (h + 1) * CHUNK])
-                if (u, h) == (0, 0):
-                    for quad in range(4):
-                        nc.sync.dma_start(
-                            scale_pool[32 * quad : 32 * quad + 4, :], scale_rows[4 * quad : 4 * quad + 4, :]
-                        )
-                    nc.sync.dma_start(c_list[:], offs2)
-        q_raw = sb.tile([P, PACK, NQ], F32, name="q_raw", tag="q_then_c", align_bytes=64)
+        c_raw0 = sb.tile([P, 2, 512], F32, name="c_raw0")
+        nc.sync.dma_start(c_raw0[:], c_rows[:, 0:2, 0:512])
+        nc.sync.dma_start(k_list[:], offs)
+        nc.sync.dma_start(scale_pool[0:P:8, :], scale_rows)
+        nc.sync.dma_start(c_list[:], offs2)
+        c_raw1 = sb.tile([P, 2, 512], F32, name="c_raw1")
+        nc.sync.dma_start(c_raw1[:], c_rows[:, 0:2, 512:1024])
+        c_raw2 = sb.tile([P, 2, 512], F32, name="c_raw2")
+        nc.sync.dma_start(c_raw2[:], c_rows[:, 2:4, 0:512])
+        c_raw3 = sb.tile([P, 2, 512], F32, name="c_raw3")
+        nc.sync.dma_start(c_raw3[:], c_rows[:, 2:4, 512:1024])
+        q_raw = sb.tile([P, PACK, NQ], F32, name="q_raw", align_bytes=64)
         nc.sync.dma_start(q_raw[:], qT[0].rearrange("(p t) n -> p t n", t=PACK))
-        k_pool = sb.tile([P, T], I32, name="k_pool", tag="k_then_neg", align_bytes=64)
+        k_pool = late.tile([P, T], I32, name="k_pool", offset=0, align_bytes=64)
         nc.sync.dma_start(k_pool[:], k_words[0].rearrange("p n r -> p (n r)").bitcast(I32))
 
-        k_scale = sb.tile([P, N], U8, name="k_scale", align_bytes=64)
-        nc.vector.tensor_copy(k_scale[:], scale_pool[:].bitcast(U8).indirect(k_list[:]))
+        picked = sb.tile([P, N], U8, name="picked", align_bytes=64)
+        nc.vector.tensor_copy(picked[:], scale_pool[:].bitcast(U8).indirect(k_list[:]))
+        plane = sb.tile([P, N // 4], I32, name="plane", align_bytes=64)
+        nc.vector.memset(plane[:], 0)
+        for quad in range(4):
+            nc.sync.dma_start(plane[32 * quad : 32 * quad + 4, :], picked[:].bitcast(I32)[32 * quad : 32 * quad + 32 : 8, :])
+        k_scale = plane[:].bitcast(U8)
 
         c_pairs = sb.tile([P, 2, N], U32, name="c_pairs", align_bytes=64)
-        for u in range(2):
-            pair_pool = sb.tile([P, TC, 2], BF16, name="pair_pool%d" % u, align_bytes=64)
-            for h in range(TC // CHUNK):
-                src = c_raw[u, h][:].rearrange("p e n -> p n e")
-                dst = pair_pool[:, h * CHUNK : (h + 1) * CHUNK, :]
-                if h == 1:
-                    nc.vector.tensor_copy(dst[:, :LAST_ON_VECTOR, :], src[:, :LAST_ON_VECTOR, :])
-                    nc.scalar.copy(dst[:, LAST_ON_VECTOR:, :], src[:, LAST_ON_VECTOR:, :])
-                else:
-                    nc.scalar.copy(dst, src)
-            window = pair_pool[:].rearrange("p n e -> p (n e)").bitcast(U32)
-            if u == 0:
-                nc.vector.tensor_copy(c_pairs[:, u, :], window.indirect(c_list[:]))
-            else:
-                for h in range(2):
-                    nc.vector.tensor_copy(
-                        c_pairs[:, u, h * 256 : (h + 1) * 256], window.indirect(c_list[:, h * 16 : (h + 1) * 16])
-                    )
-
-        q_bf = sb.tile([P, NQ, PACK], BF16, name="q_bf", tag="q_then_codes", align_bytes=64)
-        nc.scalar.copy(
-            q_bf[:].rearrange("p (c i) t -> p c t i", i=4), q_raw[:].rearrange("p t (c i) -> p c t i", i=4)
-        )
-
-        c_scale = sb.tile([P, N], U8, name="c_scale", align_bytes=64)
-        half = N // 2
-        c_bf = [
-            sb.tile([P, half * PACK], BF16, name="c_bf0", align_bytes=64),
-            sb.tile([P, half * PACK], BF16, name="c_bf1", tag="q_then_c", align_bytes=64),
-        ]
-        for h, engine_copy, word in ((0, nc.vector.tensor_copy, I32), (1, nc.scalar.copy, F32)):
-            cols = slice(h * half, (h + 1) * half)
-            engine_copy(
-                c_bf[h][:].bitcast(word).rearrange("p (n u) -> p n u", u=2),
-                c_pairs[:].bitcast(word).rearrange("p u n -> p n u")[:, cols],
-            )
-        q_code = sb.tile([P, NQ], U32, name="q_code", align_bytes=64)
-        q_scale = sb.tile([P, NQ], U8, name="q_scale", align_bytes=64)
-        nc.vector.quantize_mx(
-            out=q_code[:].bitcast(FP8X4), scales=q_scale[:], in_=q_bf[:].rearrange("p n t -> p (n t)")
-        )
-        c_code = sb.tile([P, N], U32, name="c_code", tag="q_then_codes", align_bytes=64)
+        pair_pool0 = sb.tile([P, TC, 2], BF16, name="pair_pool0", align_bytes=64)
+        nc.scalar.copy(pair_pool0[:, 0:512, :], c_raw0[:].rearrange("p e n -> p n e")[:, 0:, :])
+        nc.vector.tensor_copy(pair_pool0[:, 512:864, :], c_raw1[:].rearrange("p e n -> p n e")[:, :352, :])
+        nc.scalar.copy(pair_pool0[:, 864:1024, :], c_raw1[:].rearrange("p e n -> p n e")[:, 352:, :])
+        window = pair_pool0[:].rearrange("p n e -> p (n e)").bitcast(U32)
+        nc.vector.tensor_copy(c_pairs[:, 0, :], window.indirect(c_list[:]))
+        pair_pool1 = sb.tile([P, TC, 2], BF16, name="pair_pool1", align_bytes=64)
+        nc.scalar.copy(pair_pool1[:, 0:512, :], c_raw2[:].rearrange("p e n -> p n e")[:, 0:, :])
+        nc.vector.tensor_copy(pair_pool1[:, 512:864, :], c_raw3[:].rearrange("p e n -> p n e")[:, :352, :])
+        nc.scalar.copy(pair_pool1[:, 864:1024, :], c_raw3[:].rearrange("p e n -> p n e")[:, 352:, :])
+        window = pair_pool1[:].rearrange("p n e -> p (n e)").bitcast(U32)
         for h in range(2):
-            cols = slice(h * half, (h + 1) * half)
-            nc.vector.quantize_mx(
-                out=c_code[:, cols].bitcast(FP8X4),
-                scales=c_scale[:, cols],
-                in_=c_bf[h][:],
+            nc.vector.tensor_copy(c_pairs[:, 1, h * HALF : (h + 1) * HALF], window.indirect(c_list[:, h * 16 : (h + 1) * 16]))
+
+        q_bf = [sb.tile([P, P, PACK], BF16, name="q_bf%d" % b, align_bytes=64) for b in range(2)]
+        for b in range(2):
+            nc.scalar.copy(
+                q_bf[b][:].rearrange("p (c i) t -> p c t i", i=4),
+                q_raw[:, :, b * P : (b + 1) * P].rearrange("p t (c i) -> p c t i", i=4),
             )
-        def scores(bank, b, h, code, scale):
-            rows = slice(b * P, (b + 1) * P)
-            cols = slice(h * half, (h + 1) * half)
+        c_bf = [sb.tile([P, HALF * PACK], BF16, name="c_bf%d" % h, align_bytes=64) for h in range(2)]
+        for h in range(2):
+            nc.vector.tensor_copy(
+                c_bf[h][:].bitcast(I32).rearrange("p (n u) -> p n u", u=2),
+                c_pairs[:].bitcast(I32).rearrange("p u n -> p n u")[:, h * HALF : (h + 1) * HALF],
+            )
+        c_code = sb.tile([P, N], U32, name="c_code", align_bytes=64)
+        c_scale = sb.tile([P, N], U8, name="c_scale", align_bytes=64)
+        q_code = [sb.tile([P, P], U32, name="q_code%d" % b, align_bytes=64) for b in range(2)]
+        q_scale = [
+            sb.tile([P, P], U8, name="q_scale0", align_bytes=64),
+            sb.tile([P, P], U8, name="q_scale1", align_bytes=64),
+        ]
+        for h in range(2):
+            cols = slice(h * HALF, (h + 1) * HALF)
+            nc.vector.quantize_mx(out=c_code[:, cols].bitcast(FP8X4), scales=c_scale[:, cols], in_=c_bf[h][:])
+
+        def quantize_q(b):
+            nc.vector.quantize_mx(
+                out=q_code[b][:].bitcast(FP8X4), scales=q_scale[b][:], in_=q_bf[b][:].rearrange("p n t -> p (n t)")
+            )
+
+        quantize_q(0)
+        quantize_q(1)
+
+        def scores(bank, b, cols, code, scale):
             nc.tensor.matmul_mx(
                 out=bank[:, cols],
-                lhsT=q_code[:, rows].bitcast(FP8X4),
-                lhsT_scale=q_scale[:, rows],
+                lhsT=q_code[b][:].bitcast(FP8X4),
+                lhsT_scale=q_scale[b][:],
                 rhs=code[:, cols].bitcast(FP8X4),
                 rhs_scale=scale[:, cols],
                 start=True,
@@ -126,62 +122,65 @@ def tile_attend_locmix_topk_kernel(tc, qT, k_words, k_scales, cT, offs, offs2, o
 
         z_bank = [psum.tile([P, N], F32, name="z%d" % b) for b in range(2)]
         a_bank = [psum.tile([P, N], F32, name="a%d" % b) for b in range(2)]
-        for b in range(2):
-            for h in range(2):
-                scores(z_bank[b], b, h, c_code, c_scale)
-
         k_code = sb.tile([P, N], U32, name="k_code", align_bytes=64)
         for h in range(2):
             nc.vector.tensor_copy(
-                k_code[:, h * half : (h + 1) * half], k_pool[:].bitcast(U32).indirect(k_list[:, h * 16 : (h + 1) * 16])
+                k_code[:, h * HALF : (h + 1) * HALF], k_pool[:].bitcast(U32).indirect(k_list[:, h * 16 : (h + 1) * 16])
             )
-        for h in range(2):
-            for b in range(2):
-                scores(a_bank[b], b, h, k_code, k_scale)
+        halves = [slice(0, HALF), slice(HALF, N)]
+        for b, pieces in ((0, halves), (1, halves)):
+            for cols in pieces:
+                scores(z_bank[b], b, cols, c_code, c_scale)
+            for cols in pieces:
+                scores(a_bank[b], b, cols, k_code, k_scale)
+
 
         def col(name):
             return sb.tile([P, 1], F32, name=name)
 
-        neg = [
-            sb.tile([P, N + 1], F32, name="neg0"),
-            sb.tile([P, N + 1], F32, name="neg1", tag="k_then_neg", align_bytes=64),
-        ]
-        e_z, e_a, l_a = [], [], []
-        l_z = sb.tile([P, 2], F32, name="l_z")
-        l_z1 = sb.tile([P, 2], F32, name="l_z1")
-        for b in range(2):
+        neg_t = [late.tile([P, N + 1], F32, name="neg%d" % b, offset=2560 * b, align_bytes=64) for b in range(2)]
+        neg = [t[:] for t in neg_t]
+        e_z = [sb.tile([P, N], F32, name="e_z%d" % b) for b in range(2)]
+        e_a = [sb.tile([P, N], F32, name="e_a%d" % b) for b in range(2)]
+        l_z, l_a, neg_m, neg_h, total, inv = (
+            [col("%s%d" % (name, b)) for b in range(2)]
+            for name in ("l_z", "l_a", "neg_m", "neg_h", "total", "inv")
+        )
+        shift = [col("shift%d" % b)[:] for b in range(2)]
+
+        def max_z(b):
             neg_mz = neg[b][:, N : N + 1]
             nc.vector.tensor_reduce(neg_mz, z_bank[b][:], mybir.AxisListType.X, ALU.max, negate=True)
-            e_z.append(sb.tile([P, N], F32, name="e_z%d" % b))
-            nc.scalar.activation(e_z[b][:], z_bank[b][:], ACT.Exp, bias=neg_mz, accum_out=l_z[:, b : b + 1])
-            nc.scalar.activation(l_z1[:, b : b + 1], l_z[:, b : b + 1], ACT.Identity, bias=-1.0)
-        for b in range(2):
-            neg_a = neg[b][:]
-            neg_mz = neg[b][:, N : N + 1]
-            neg_m = col("neg_m%d" % b)
-            nc.vector.tensor_scalar(neg_a[:, :N], a_bank[b][:], -1.0, neg_mz, ALU.mult, ALU.min, accum_out=neg_m[:])
-            e_a.append(sb.tile([P, N + 1], F32, name="e_a%d" % b))
-            l_a.append(col("l_a%d" % b))
-            nc.scalar.activation(e_a[b][:], neg_a, ACT.Exp, bias=neg_m[:], scale=-1.0, accum_out=l_a[b][:])
+            nc.scalar.activation(e_z[b][:], z_bank[b][:], ACT.Exp, bias=neg_mz, accum_out=l_z[b][:])
 
-        shift = [e_a[b][:, N : N + 1] for b in range(2)]
-        total = [col("total%d" % b) for b in range(2)]
-        inv = [col("inv%d" % b) for b in range(2)]
-        y = [
-            sb.tile([P, N], F32, name="y0", tag="k_then_neg", align_bytes=64),
-            sb.tile([P, N], F32, name="y1"),
-        ]
+        def max_a(b, cols, start, result):
+            nc.vector.tensor_scalar(neg[b][:, cols], a_bank[b][:, cols], -1.0, start, ALU.mult, ALU.min, accum_out=result)
+
+        def exp_a(b):
+            nc.scalar.activation(shift[b], neg[b][:, N : N + 1], ACT.Exp, bias=neg_m[b][:], scale=-1.0)
+            nc.scalar.activation(e_a[b][:], neg[b][:, :N], ACT.Exp, bias=neg_m[b][:], scale=-1.0, accum_out=l_a[b][:])
 
         def row_sum(b):
-            nc.vector.tensor_scalar(total[b][:], l_z1[:, b : b + 1], shift[b], l_a[b][:], ALU.mult, ALU.add)
+            nc.vector.tensor_scalar(total[b][:], l_z[b][:], shift[b], l_a[b][:], ALU.mult, ALU.add)
 
-        def weights(b):
-            nc.vector.tensor_scalar(y[b][:], e_z[b][:], shift[b], inv[b][:], ALU.mult, ALU.mult)
-            nc.sync.dma_start(out[0, b * P : (b + 1) * P, :], y[b][:])
+        def invert(b):
+            nc.vector.reciprocal(inv[b][:], total[b][:])
 
+        def weights(b, lo, hi, queue):
+            y = sb.tile([P, hi - lo], F32, name="y%d_%d" % (b, lo))
+            nc.vector.tensor_scalar(y[:], e_z[b][:, lo:hi], shift[b], inv[b][:], ALU.mult, ALU.mult)
+            queue.dma_start(out[0, b * P : (b + 1) * P, lo:hi], y[:])
+
+        max_z(0)
+        max_z(1)
+        max_a(0, slice(0, N), neg[0][:, N : N + 1], neg_m[0][:])
+        exp_a(0)
+        max_a(1, slice(0, N), neg[1][:, N : N + 1], neg_m[1][:])
+        exp_a(1)
         row_sum(0)
-        nc.vector.reciprocal(inv[0][:], total[0][:])
+        invert(0)
         row_sum(1)
-        weights(0)
-        nc.vector.reciprocal(inv[1][:], total[1][:])
-        weights(1)
+        weights(0, 0, N, nc.sync)
+        invert(1)
+        weights(1, 0, 256, nc.sync)
+        weights(1, 256, N, nc.sync)

@@ -29,7 +29,7 @@ def tile_attend_locmix_topk_kernel(tc, qT, k_words, k_scales, cT, offs, offs2, o
         psum = ctx.enter_context(tc.psum_pool(name="psum", bufs=1))
 
         scale_pool = sb.tile([P, T // 4], I32, name="scale_pool", align_bytes=64)
-        nc.vector.memset(scale_pool[:], 0)
+        nc.vector.memset(scale_pool[:112, :], 0)
         warm = sb.tile([P, 1], F32, name="warm")
         warm_out = sb.tile([P, 1], F32, name="warm_out")
         nc.vector.memset(warm[:], 0.0)
@@ -39,41 +39,38 @@ def tile_attend_locmix_topk_kernel(tc, qT, k_words, k_scales, cT, offs, offs2, o
         k_list = lists.tile([P, N // 16], U16, name="k_list")
         c_rows = cT.rearrange("(p t) n -> p t n", t=PACK)
         scale_rows = k_scales[0].bitcast(I32)
-        c_raw0 = sb.tile([P, 2, 512], F32, name="c_raw0")
-        nc.sync.dma_start(c_raw0[:], c_rows[:, 0:2, 0:512])
+        nc.sync.dma_start(scale_pool[112:, :], scale_rows)
         nc.sync.dma_start(k_list[:], offs)
-        nc.sync.dma_start(scale_pool[0:P:8, :], scale_rows)
+        c_raw0 = sb.tile([P, 2, 1024], F32, name="c_raw0")
+        nc.sync.dma_start(c_raw0[:], c_rows[:, 0:2, 0:1024])
         nc.sync.dma_start(c_list[:], offs2)
         c_raw1 = sb.tile([P, 2, 512], F32, name="c_raw1")
-        nc.sync.dma_start(c_raw1[:], c_rows[:, 0:2, 512:1024])
+        nc.sync.dma_start(c_raw1[:], c_rows[:, 2:4, 0:512])
         c_raw2 = sb.tile([P, 2, 512], F32, name="c_raw2")
-        nc.sync.dma_start(c_raw2[:], c_rows[:, 2:4, 0:512])
-        c_raw3 = sb.tile([P, 2, 512], F32, name="c_raw3")
-        nc.sync.dma_start(c_raw3[:], c_rows[:, 2:4, 512:1024])
+        nc.sync.dma_start(c_raw2[:], c_rows[:, 2:4, 512:1024])
         q_raw = sb.tile([P, PACK, NQ], F32, name="q_raw", align_bytes=64)
         nc.sync.dma_start(q_raw[:], qT[0].rearrange("(p t) n -> p t n", t=PACK))
-        k_pool = late.tile([P, T], I32, name="k_pool", offset=0, align_bytes=64)
+        k_pool = sb.tile([P, T], I32, name="k_pool", align_bytes=64)
         nc.sync.dma_start(k_pool[:], k_words[0].rearrange("p n r -> p (n r)").bitcast(I32))
 
-        picked = sb.tile([P, N], U8, name="picked", align_bytes=64)
+        picked = late.tile([P, N], U8, name="picked", offset=1792, align_bytes=64)
         nc.vector.tensor_copy(picked[:], scale_pool[:].bitcast(U8).indirect(k_list[:]))
         plane = sb.tile([P, N // 4], I32, name="plane", align_bytes=64)
         nc.vector.memset(plane[:], 0)
         for quad in range(4):
-            nc.sync.dma_start(plane[32 * quad : 32 * quad + 4, :], picked[:].bitcast(I32)[32 * quad : 32 * quad + 32 : 8, :])
+            nc.sync.dma_start(plane[32 * quad : 32 * quad + 4, :], picked[:].bitcast(I32)[112 + 4 * quad : 116 + 4 * quad, :])
         k_scale = plane[:].bitcast(U8)
 
         c_pairs = sb.tile([P, 2, N], U32, name="c_pairs", align_bytes=64)
         pair_pool0 = sb.tile([P, TC, 2], BF16, name="pair_pool0", align_bytes=64)
-        nc.scalar.copy(pair_pool0[:, 0:512, :], c_raw0[:].rearrange("p e n -> p n e")[:, 0:, :])
-        nc.vector.tensor_copy(pair_pool0[:, 512:864, :], c_raw1[:].rearrange("p e n -> p n e")[:, :352, :])
-        nc.scalar.copy(pair_pool0[:, 864:1024, :], c_raw1[:].rearrange("p e n -> p n e")[:, 352:, :])
+        nc.vector.tensor_copy(pair_pool0[:, 0:672, :], c_raw0[:].rearrange("p e n -> p n e")[:, :672, :])
+        nc.scalar.copy(pair_pool0[:, 672:1024, :], c_raw0[:].rearrange("p e n -> p n e")[:, 672:, :])
         window = pair_pool0[:].rearrange("p n e -> p (n e)").bitcast(U32)
         nc.vector.tensor_copy(c_pairs[:, 0, :], window.indirect(c_list[:]))
         pair_pool1 = sb.tile([P, TC, 2], BF16, name="pair_pool1", align_bytes=64)
-        nc.scalar.copy(pair_pool1[:, 0:512, :], c_raw2[:].rearrange("p e n -> p n e")[:, 0:, :])
-        nc.vector.tensor_copy(pair_pool1[:, 512:864, :], c_raw3[:].rearrange("p e n -> p n e")[:, :352, :])
-        nc.scalar.copy(pair_pool1[:, 864:1024, :], c_raw3[:].rearrange("p e n -> p n e")[:, 352:, :])
+        nc.scalar.copy(pair_pool1[:, 0:512, :], c_raw1[:].rearrange("p e n -> p n e")[:, 0:, :])
+        nc.vector.tensor_copy(pair_pool1[:, 512:864, :], c_raw2[:].rearrange("p e n -> p n e")[:, :352, :])
+        nc.scalar.copy(pair_pool1[:, 864:1024, :], c_raw2[:].rearrange("p e n -> p n e")[:, 352:, :])
         window = pair_pool1[:].rearrange("p n e -> p (n e)").bitcast(U32)
         for h in range(2):
             nc.vector.tensor_copy(c_pairs[:, 1, h * HALF : (h + 1) * HALF], window.indirect(c_list[:, h * 16 : (h + 1) * 16]))
@@ -138,7 +135,10 @@ def tile_attend_locmix_topk_kernel(tc, qT, k_words, k_scales, cT, offs, offs2, o
         def col(name):
             return sb.tile([P, 1], F32, name=name)
 
-        neg_t = [late.tile([P, N + 1], F32, name="neg%d" % b, offset=2560 * b, align_bytes=64) for b in range(2)]
+        neg_t = [
+            late.tile([P, N + 1], F32, name="neg0", offset=0, align_bytes=64),
+            late.tile([P, N + 1], F32, name="neg1", offset=2112, align_bytes=64),
+        ]
         neg = [t[:] for t in neg_t]
         e_z = [sb.tile([P, N], F32, name="e_z%d" % b) for b in range(2)]
         e_a = [sb.tile([P, N], F32, name="e_a%d" % b) for b in range(2)]

@@ -30,10 +30,6 @@ def tile_attend_locmix_topk_kernel(tc, qT, k_words, k_scales, cT, offs, offs2, o
 
         scale_pool = sb.tile([P, T // 4], I32, name="scale_pool", align_bytes=64)
         nc.vector.memset(scale_pool[:112, :], 0)
-        warm = sb.tile([P, 1], F32, name="warm")
-        warm_out = sb.tile([P, 1], F32, name="warm_out")
-        nc.vector.memset(warm[:], 0.0)
-        nc.scalar.activation(warm_out[:], warm[:], ACT.Exp)
 
         c_list = lists.tile([P, N // 16], U16, name="c_list")
         k_list = lists.tile([P, N // 16], U16, name="k_list")
@@ -41,13 +37,15 @@ def tile_attend_locmix_topk_kernel(tc, qT, k_words, k_scales, cT, offs, offs2, o
         scale_rows = k_scales[0].bitcast(I32)
         nc.sync.dma_start(scale_pool[112:, :], scale_rows)
         nc.sync.dma_start(k_list[:], offs)
-        c_raw0 = sb.tile([P, 2, 1024], F32, name="c_raw0")
-        nc.sync.dma_start(c_raw0[:], c_rows[:, 0:2, 0:1024])
+        c_raw0 = sb.tile([P, 2, 768], F32, name="c_raw0")
+        nc.sync.dma_start(c_raw0[:], c_rows[:, 0:2, 0:768])
         nc.sync.dma_start(c_list[:], offs2)
-        c_raw1 = sb.tile([P, 2, 512], F32, name="c_raw1")
-        nc.sync.dma_start(c_raw1[:], c_rows[:, 2:4, 0:512])
+        c_raw1 = sb.tile([P, 2, 256], F32, name="c_raw1")
+        nc.sync.dma_start(c_raw1[:], c_rows[:, 0:2, 768:1024])
         c_raw2 = sb.tile([P, 2, 512], F32, name="c_raw2")
-        nc.sync.dma_start(c_raw2[:], c_rows[:, 2:4, 512:1024])
+        nc.sync.dma_start(c_raw2[:], c_rows[:, 2:4, 0:512])
+        c_raw3 = sb.tile([P, 2, 512], F32, name="c_raw3")
+        nc.sync.dma_start(c_raw3[:], c_rows[:, 2:4, 512:1024])
         q_raw = sb.tile([P, PACK, NQ], F32, name="q_raw", align_bytes=64)
         nc.sync.dma_start(q_raw[:], qT[0].rearrange("(p t) n -> p t n", t=PACK))
         k_pool = sb.tile([P, T], I32, name="k_pool", align_bytes=64)
@@ -63,14 +61,37 @@ def tile_attend_locmix_topk_kernel(tc, qT, k_words, k_scales, cT, offs, offs2, o
 
         c_pairs = sb.tile([P, 2, N], U32, name="c_pairs", align_bytes=64)
         pair_pool0 = sb.tile([P, TC, 2], BF16, name="pair_pool0", align_bytes=64)
-        nc.vector.tensor_copy(pair_pool0[:, 0:672, :], c_raw0[:].rearrange("p e n -> p n e")[:, :672, :])
-        nc.scalar.copy(pair_pool0[:, 672:1024, :], c_raw0[:].rearrange("p e n -> p n e")[:, 672:, :])
+        nc.vector.tensor_copy(
+            pair_pool0[:, 0:576, :].rearrange("p (c i) e -> p c e i", i=4),
+            c_raw0[:, :, :576].rearrange("p e (c i) -> p c e i", i=4),
+        )
+        nc.scalar.copy(
+            pair_pool0[:, 576:768, :].rearrange("p (c i) e -> p c e i", i=4),
+            c_raw0[:, :, 576:].rearrange("p e (c i) -> p c e i", i=4),
+        )
+        nc.vector.tensor_copy(
+            pair_pool0[:, 768:1024, :].rearrange("p (c i) e -> p c e i", i=4),
+            c_raw1[:, :, :256].rearrange("p e (c i) -> p c e i", i=4),
+        )
         window = pair_pool0[:].rearrange("p n e -> p (n e)").bitcast(U32)
         nc.vector.tensor_copy(c_pairs[:, 0, :], window.indirect(c_list[:]))
         pair_pool1 = sb.tile([P, TC, 2], BF16, name="pair_pool1", align_bytes=64)
-        nc.scalar.copy(pair_pool1[:, 0:512, :], c_raw1[:].rearrange("p e n -> p n e")[:, 0:, :])
-        nc.vector.tensor_copy(pair_pool1[:, 512:864, :], c_raw2[:].rearrange("p e n -> p n e")[:, :352, :])
-        nc.scalar.copy(pair_pool1[:, 864:1024, :], c_raw2[:].rearrange("p e n -> p n e")[:, 352:, :])
+        nc.vector.tensor_copy(
+            pair_pool1[:, 0:160, :].rearrange("p (c i) e -> p c e i", i=4),
+            c_raw2[:, :, :160].rearrange("p e (c i) -> p c e i", i=4),
+        )
+        nc.scalar.copy(
+            pair_pool1[:, 160:512, :].rearrange("p (c i) e -> p c e i", i=4),
+            c_raw2[:, :, 160:].rearrange("p e (c i) -> p c e i", i=4),
+        )
+        nc.vector.tensor_copy(
+            pair_pool1[:, 512:848, :].rearrange("p (c i) e -> p c e i", i=4),
+            c_raw3[:, :, :336].rearrange("p e (c i) -> p c e i", i=4),
+        )
+        nc.scalar.copy(
+            pair_pool1[:, 848:1024, :].rearrange("p (c i) e -> p c e i", i=4),
+            c_raw3[:, :, 336:].rearrange("p e (c i) -> p c e i", i=4),
+        )
         window = pair_pool1[:].rearrange("p n e -> p (n e)").bitcast(U32)
         for h in range(2):
             nc.vector.tensor_copy(c_pairs[:, 1, h * HALF : (h + 1) * HALF], window.indirect(c_list[:, h * 16 : (h + 1) * 16]))
@@ -84,8 +105,8 @@ def tile_attend_locmix_topk_kernel(tc, qT, k_words, k_scales, cT, offs, offs2, o
         c_bf = [sb.tile([P, HALF * PACK], BF16, name="c_bf%d" % h, align_bytes=64) for h in range(2)]
         for h in range(2):
             nc.vector.tensor_copy(
-                c_bf[h][:].bitcast(I32).rearrange("p (n u) -> p n u", u=2),
-                c_pairs[:].bitcast(I32).rearrange("p u n -> p n u")[:, h * HALF : (h + 1) * HALF],
+                c_bf[h][:].bitcast(I32).rearrange("p (c i u) -> p c u i", i=4, u=2),
+                c_pairs[:, :, h * HALF : (h + 1) * HALF].bitcast(I32).rearrange("p u (c i) -> p c u i", i=4),
             )
         c_code = sb.tile([P, N], U32, name="c_code", align_bytes=64)
         c_scale = sb.tile([P, N], U8, name="c_scale", align_bytes=64)
@@ -183,4 +204,4 @@ def tile_attend_locmix_topk_kernel(tc, qT, k_words, k_scales, cT, offs, offs2, o
         weights(0, 0, N, nc.sync)
         invert(1)
         weights(1, 0, 256, nc.sync)
-        weights(1, 256, N, nc.sync)
+        weights(1, 256, N, nc.scalar)

@@ -29,19 +29,19 @@ def tile_attend_locmix_topk_kernel(tc, qT, k_words, k_scales, cT, offs, offs2, o
         psum = ctx.enter_context(tc.psum_pool(name="psum", bufs=1))
 
         scale_pool = sb.tile([P, T // 4], I32, name="scale_pool", align_bytes=64)
-        nc.vector.memset(scale_pool[:112, :], 0)
+        nc.vector.memset(scale_pool[:], 0)
 
         c_list = lists.tile([P, N // 16], U16, name="c_list")
         k_list = lists.tile([P, N // 16], U16, name="k_list")
         c_rows = cT.rearrange("(p t) n -> p t n", t=PACK)
         scale_rows = k_scales[0].bitcast(I32)
-        nc.sync.dma_start(scale_pool[112:, :], scale_rows)
+        c_raw0 = sb.tile([P, 2, 512], F32, name="c_raw0")
+        nc.sync.dma_start(c_raw0[:], c_rows[:, 0:2, 0:512])
         nc.sync.dma_start(k_list[:], offs)
-        c_raw0 = sb.tile([P, 2, 768], F32, name="c_raw0")
-        nc.sync.dma_start(c_raw0[:], c_rows[:, 0:2, 0:768])
+        nc.sync.dma_start(scale_pool[32:96:4, :], scale_rows)
         nc.sync.dma_start(c_list[:], offs2)
-        c_raw1 = sb.tile([P, 2, 256], F32, name="c_raw1")
-        nc.sync.dma_start(c_raw1[:], c_rows[:, 0:2, 768:1024])
+        c_raw1 = sb.tile([P, 2, 512], F32, name="c_raw1")
+        nc.sync.dma_start(c_raw1[:], c_rows[:, 0:2, 512:1024])
         c_raw2 = sb.tile([P, 2, 512], F32, name="c_raw2")
         nc.sync.dma_start(c_raw2[:], c_rows[:, 2:4, 0:512])
         c_raw3 = sb.tile([P, 2, 512], F32, name="c_raw3")
@@ -56,52 +56,46 @@ def tile_attend_locmix_topk_kernel(tc, qT, k_words, k_scales, cT, offs, offs2, o
         plane = sb.tile([P, N // 4], I32, name="plane", align_bytes=64)
         nc.vector.memset(plane[:], 0)
         for quad in range(4):
-            nc.sync.dma_start(plane[32 * quad : 32 * quad + 4, :], picked[:].bitcast(I32)[112 + 4 * quad : 116 + 4 * quad, :])
+            nc.sync.dma_start(plane[32 * quad : 32 * quad + 4, :], picked[:].bitcast(I32)[32 + 16 * quad : 48 + 16 * quad : 4, :])
         k_scale = plane[:].bitcast(U8)
 
         c_pairs = sb.tile([P, 2, N], U32, name="c_pairs", align_bytes=64)
         pair_pool0 = sb.tile([P, TC, 2], BF16, name="pair_pool0", align_bytes=64)
+        nc.scalar.copy(
+            pair_pool0[:, 0:512, :].rearrange("p (c i) e -> p c e i", i=4),
+            c_raw0[:, :, 0:].rearrange("p e (c i) -> p c e i", i=4),
+        )
         nc.vector.tensor_copy(
-            pair_pool0[:, 0:576, :].rearrange("p (c i) e -> p c e i", i=4),
-            c_raw0[:, :, :576].rearrange("p e (c i) -> p c e i", i=4),
+            pair_pool0[:, 512:864, :].rearrange("p (c i) e -> p c e i", i=4),
+            c_raw1[:, :, :352].rearrange("p e (c i) -> p c e i", i=4),
         )
         nc.scalar.copy(
-            pair_pool0[:, 576:768, :].rearrange("p (c i) e -> p c e i", i=4),
-            c_raw0[:, :, 576:].rearrange("p e (c i) -> p c e i", i=4),
-        )
-        nc.vector.tensor_copy(
-            pair_pool0[:, 768:1024, :].rearrange("p (c i) e -> p c e i", i=4),
-            c_raw1[:, :, :256].rearrange("p e (c i) -> p c e i", i=4),
+            pair_pool0[:, 864:1024, :].rearrange("p (c i) e -> p c e i", i=4),
+            c_raw1[:, :, 352:].rearrange("p e (c i) -> p c e i", i=4),
         )
         window = pair_pool0[:].rearrange("p n e -> p (n e)").bitcast(U32)
         nc.vector.tensor_copy(c_pairs[:, 0, :], window.indirect(c_list[:]))
         pair_pool1 = sb.tile([P, TC, 2], BF16, name="pair_pool1", align_bytes=64)
-        nc.vector.tensor_copy(
-            pair_pool1[:, 0:160, :].rearrange("p (c i) e -> p c e i", i=4),
-            c_raw2[:, :, :160].rearrange("p e (c i) -> p c e i", i=4),
-        )
         nc.scalar.copy(
-            pair_pool1[:, 160:512, :].rearrange("p (c i) e -> p c e i", i=4),
-            c_raw2[:, :, 160:].rearrange("p e (c i) -> p c e i", i=4),
+            pair_pool1[:, 0:512, :].rearrange("p (c i) e -> p c e i", i=4),
+            c_raw2[:, :, 0:].rearrange("p e (c i) -> p c e i", i=4),
         )
         nc.vector.tensor_copy(
-            pair_pool1[:, 512:848, :].rearrange("p (c i) e -> p c e i", i=4),
-            c_raw3[:, :, :336].rearrange("p e (c i) -> p c e i", i=4),
+            pair_pool1[:, 512:864, :].rearrange("p (c i) e -> p c e i", i=4),
+            c_raw3[:, :, :352].rearrange("p e (c i) -> p c e i", i=4),
         )
         nc.scalar.copy(
-            pair_pool1[:, 848:1024, :].rearrange("p (c i) e -> p c e i", i=4),
-            c_raw3[:, :, 336:].rearrange("p e (c i) -> p c e i", i=4),
+            pair_pool1[:, 864:1024, :].rearrange("p (c i) e -> p c e i", i=4),
+            c_raw3[:, :, 352:].rearrange("p e (c i) -> p c e i", i=4),
         )
         window = pair_pool1[:].rearrange("p n e -> p (n e)").bitcast(U32)
         for h in range(2):
             nc.vector.tensor_copy(c_pairs[:, 1, h * HALF : (h + 1) * HALF], window.indirect(c_list[:, h * 16 : (h + 1) * 16]))
 
-        q_bf = [sb.tile([P, P, PACK], BF16, name="q_bf%d" % b, align_bytes=64) for b in range(2)]
-        for b in range(2):
-            nc.scalar.copy(
-                q_bf[b][:].rearrange("p (c i) t -> p c t i", i=4),
-                q_raw[:, :, b * P : (b + 1) * P].rearrange("p t (c i) -> p c t i", i=4),
-            )
+        q_bf = sb.tile([P, NQ, PACK], BF16, name="q_bf", align_bytes=64)
+        nc.scalar.copy(
+            q_bf[:].rearrange("p (c i) t -> p c t i", i=4), q_raw[:].rearrange("p t (c i) -> p c t i", i=4)
+        )
         c_bf = [sb.tile([P, HALF * PACK], BF16, name="c_bf%d" % h, align_bytes=64) for h in range(2)]
         for h in range(2):
             nc.vector.tensor_copy(
@@ -110,28 +104,21 @@ def tile_attend_locmix_topk_kernel(tc, qT, k_words, k_scales, cT, offs, offs2, o
             )
         c_code = sb.tile([P, N], U32, name="c_code", align_bytes=64)
         c_scale = sb.tile([P, N], U8, name="c_scale", align_bytes=64)
-        q_code = [sb.tile([P, P], U32, name="q_code%d" % b, align_bytes=64) for b in range(2)]
-        q_scale = [
-            sb.tile([P, P], U8, name="q_scale0", align_bytes=64),
-            sb.tile([P, P], U8, name="q_scale1", align_bytes=64),
-        ]
+        q_code = sb.tile([P, NQ], U32, name="q_code", align_bytes=64)
+        q_scale = sb.tile([P, NQ], U8, name="q_scale", align_bytes=64)
         for h in range(2):
             cols = slice(h * HALF, (h + 1) * HALF)
             nc.vector.quantize_mx(out=c_code[:, cols].bitcast(FP8X4), scales=c_scale[:, cols], in_=c_bf[h][:])
 
-        def quantize_q(b):
-            nc.vector.quantize_mx(
-                out=q_code[b][:].bitcast(FP8X4), scales=q_scale[b][:], in_=q_bf[b][:].rearrange("p n t -> p (n t)")
-            )
-
-        quantize_q(0)
-        quantize_q(1)
+        nc.vector.quantize_mx(
+            out=q_code[:].bitcast(FP8X4), scales=q_scale[:], in_=q_bf[:].rearrange("p n t -> p (n t)")
+        )
 
         def scores(bank, b, cols, code, scale):
             nc.tensor.matmul_mx(
                 out=bank[:, cols],
-                lhsT=q_code[b][:].bitcast(FP8X4),
-                lhsT_scale=q_scale[b][:],
+                lhsT=q_code[:, b * P : (b + 1) * P].bitcast(FP8X4),
+                lhsT_scale=q_scale[:, b * P : (b + 1) * P],
                 rhs=code[:, cols].bitcast(FP8X4),
                 rhs_scale=scale[:, cols],
                 start=True,
@@ -158,7 +145,7 @@ def tile_attend_locmix_topk_kernel(tc, qT, k_words, k_scales, cT, offs, offs2, o
 
         neg_t = [
             late.tile([P, N + 1], F32, name="neg0", offset=0, align_bytes=64),
-            late.tile([P, N + 1], F32, name="neg1", offset=2112, align_bytes=64),
+            late.tile([P, N + 1], F32, name="neg1", offset=2240, align_bytes=64),
         ]
         neg = [t[:] for t in neg_t]
         e_z = [sb.tile([P, N], F32, name="e_z%d" % b) for b in range(2)]

@@ -17,7 +17,14 @@ ACT = mybir.ActivationFunctionType
 
 P = 128
 PACK = 4
+BLOCKS = NQ // P
 HALF = N // 2
+HALVES = (slice(0, HALF), slice(HALF, N))
+LIST_HALVES = (slice(0, HALF // 16), slice(HALF // 16, N // 16))
+CHUNK = TC // 2
+LAST_ON_VECTOR = 352
+SCALE_FIRST, SCALE_STEP = 32, 4
+PICKED_AT, Q_RAW_AT = 0, 512
 
 
 def tile_attend_locmix_topk_kernel(tc, qT, k_words, k_scales, cT, offs, offs2, out):
@@ -25,7 +32,7 @@ def tile_attend_locmix_topk_kernel(tc, qT, k_words, k_scales, cT, offs, offs2, o
     with ExitStack() as ctx:
         lists = ctx.enter_context(tc.tile_pool(name="lists", bufs=1))
         sb = ctx.enter_context(tc.tile_pool(name="sb", bufs=1))
-        late = ctx.enter_context(tc.tile_pool(name="late", bufs=1))
+        shared = ctx.enter_context(tc.tile_pool(name="shared", bufs=1))
         psum = ctx.enter_context(tc.psum_pool(name="psum", bufs=1))
 
         scale_pool = sb.tile([P, T // 4], I32, name="scale_pool", align_bytes=64)
@@ -34,161 +41,144 @@ def tile_attend_locmix_topk_kernel(tc, qT, k_words, k_scales, cT, offs, offs2, o
         c_list = lists.tile([P, N // 16], U16, name="c_list")
         k_list = lists.tile([P, N // 16], U16, name="k_list")
         c_rows = cT.rearrange("(p t) n -> p t n", t=PACK)
-        scale_rows = k_scales[0].bitcast(I32)
-        c_raw0 = sb.tile([P, 2, 512], F32, name="c_raw0")
-        nc.sync.dma_start(c_raw0[:], c_rows[:, 0:2, 0:512])
-        nc.sync.dma_start(k_list[:], offs)
-        nc.sync.dma_start(scale_pool[32:96:4, :], scale_rows)
-        nc.sync.dma_start(c_list[:], offs2)
-        c_raw1 = sb.tile([P, 2, 512], F32, name="c_raw1")
-        nc.sync.dma_start(c_raw1[:], c_rows[:, 0:2, 512:1024])
-        c_raw2 = sb.tile([P, 2, 512], F32, name="c_raw2")
-        nc.sync.dma_start(c_raw2[:], c_rows[:, 2:4, 0:512])
-        c_raw3 = sb.tile([P, 2, 512], F32, name="c_raw3")
-        nc.sync.dma_start(c_raw3[:], c_rows[:, 2:4, 512:1024])
-        q_raw = sb.tile([P, PACK, NQ], F32, name="q_raw", align_bytes=64)
+        c_raw = {}
+        for u in range(2):
+            for h in range(TC // CHUNK):
+                c_raw[u, h] = sb.tile([P, 2, CHUNK], F32, name="c_raw%d%d" % (u, h))
+                nc.sync.dma_start(c_raw[u, h][:], c_rows[:, 2 * u : 2 * u + 2, h * CHUNK : (h + 1) * CHUNK])
+                if (u, h) == (0, 0):
+                    nc.sync.dma_start(k_list[:], offs)
+                    nc.sync.dma_start(
+                        scale_pool[SCALE_FIRST : SCALE_FIRST + 16 * SCALE_STEP : SCALE_STEP, :],
+                        k_scales[0].bitcast(I32),
+                    )
+                    nc.sync.dma_start(c_list[:], offs2)
+        q_raw = shared.tile([P, PACK, NQ], F32, name="q_raw", offset=Q_RAW_AT, align_bytes=64)
         nc.sync.dma_start(q_raw[:], qT[0].rearrange("(p t) n -> p t n", t=PACK))
         k_pool = sb.tile([P, T], I32, name="k_pool", align_bytes=64)
         nc.sync.dma_start(k_pool[:], k_words[0].rearrange("p n r -> p (n r)").bitcast(I32))
 
-        picked = late.tile([P, N], U8, name="picked", offset=1792, align_bytes=64)
+        picked = shared.tile([P, N], U8, name="picked", offset=PICKED_AT, align_bytes=64)
         nc.vector.tensor_copy(picked[:], scale_pool[:].bitcast(U8).indirect(k_list[:]))
-        plane = sb.tile([P, N // 4], I32, name="plane", align_bytes=64)
-        nc.vector.memset(plane[:], 0)
+        k_scale_words = sb.tile([P, N // 4], I32, name="k_scale_words", align_bytes=64)
+        nc.vector.memset(k_scale_words[:], 0)
         for quad in range(4):
-            nc.sync.dma_start(plane[32 * quad : 32 * quad + 4, :], picked[:].bitcast(I32)[32 + 16 * quad : 48 + 16 * quad : 4, :])
-        k_scale = plane[:].bitcast(U8)
+            first = SCALE_FIRST + 4 * quad * SCALE_STEP
+            nc.sync.dma_start(
+                k_scale_words[32 * quad : 32 * quad + 4, :],
+                picked[:].bitcast(I32)[first : first + 4 * SCALE_STEP : SCALE_STEP, :],
+            )
+        k_scale = k_scale_words[:].bitcast(U8)
 
         c_pairs = sb.tile([P, 2, N], U32, name="c_pairs", align_bytes=64)
-        pair_pool0 = sb.tile([P, TC, 2], BF16, name="pair_pool0", align_bytes=64)
-        nc.scalar.copy(
-            pair_pool0[:, 0:512, :].rearrange("p (c i) e -> p c e i", i=4),
-            c_raw0[:, :, 0:].rearrange("p e (c i) -> p c e i", i=4),
-        )
-        nc.vector.tensor_copy(
-            pair_pool0[:, 512:864, :].rearrange("p (c i) e -> p c e i", i=4),
-            c_raw1[:, :, :352].rearrange("p e (c i) -> p c e i", i=4),
-        )
-        nc.scalar.copy(
-            pair_pool0[:, 864:1024, :].rearrange("p (c i) e -> p c e i", i=4),
-            c_raw1[:, :, 352:].rearrange("p e (c i) -> p c e i", i=4),
-        )
-        window = pair_pool0[:].rearrange("p n e -> p (n e)").bitcast(U32)
-        nc.vector.tensor_copy(c_pairs[:, 0, :], window.indirect(c_list[:]))
-        pair_pool1 = sb.tile([P, TC, 2], BF16, name="pair_pool1", align_bytes=64)
-        nc.scalar.copy(
-            pair_pool1[:, 0:512, :].rearrange("p (c i) e -> p c e i", i=4),
-            c_raw2[:, :, 0:].rearrange("p e (c i) -> p c e i", i=4),
-        )
-        nc.vector.tensor_copy(
-            pair_pool1[:, 512:864, :].rearrange("p (c i) e -> p c e i", i=4),
-            c_raw3[:, :, :352].rearrange("p e (c i) -> p c e i", i=4),
-        )
-        nc.scalar.copy(
-            pair_pool1[:, 864:1024, :].rearrange("p (c i) e -> p c e i", i=4),
-            c_raw3[:, :, 352:].rearrange("p e (c i) -> p c e i", i=4),
-        )
-        window = pair_pool1[:].rearrange("p n e -> p (n e)").bitcast(U32)
-        for h in range(2):
-            nc.vector.tensor_copy(c_pairs[:, 1, h * HALF : (h + 1) * HALF], window.indirect(c_list[:, h * 16 : (h + 1) * 16]))
+        for u in range(2):
+            pair_pool = sb.tile([P, TC, 2], BF16, name="pair_pool%d" % u, align_bytes=64)
+            for h in range(TC // CHUNK):
+                src = c_raw[u, h][:].rearrange("p e n -> p n e")
+                dst = pair_pool[:, h * CHUNK : (h + 1) * CHUNK, :]
+                cut = LAST_ON_VECTOR if h == TC // CHUNK - 1 else 0
+                if cut:
+                    nc.vector.tensor_copy(dst[:, :cut, :], src[:, :cut, :])
+                nc.scalar.copy(dst[:, cut:, :], src[:, cut:, :])
+            window = pair_pool[:].rearrange("p n e -> p (n e)").bitcast(U32)
+            if u == 0:
+                nc.vector.tensor_copy(c_pairs[:, u, :], window.indirect(c_list[:]))
+            else:
+                for cols, entries in zip(HALVES, LIST_HALVES):
+                    nc.vector.tensor_copy(c_pairs[:, u, cols], window.indirect(c_list[:, entries]))
 
         q_bf = sb.tile([P, NQ, PACK], BF16, name="q_bf", align_bytes=64)
         nc.scalar.copy(
             q_bf[:].rearrange("p (c i) t -> p c t i", i=4), q_raw[:].rearrange("p t (c i) -> p c t i", i=4)
         )
+
         c_bf = [sb.tile([P, HALF * PACK], BF16, name="c_bf%d" % h, align_bytes=64) for h in range(2)]
-        for h in range(2):
+        for h, cols in enumerate(HALVES):
             nc.vector.tensor_copy(
-                c_bf[h][:].bitcast(I32).rearrange("p (c i u) -> p c u i", i=4, u=2),
-                c_pairs[:, :, h * HALF : (h + 1) * HALF].bitcast(I32).rearrange("p u (c i) -> p c u i", i=4),
+                c_bf[h][:].bitcast(I32).rearrange("p (n u) -> p n u", u=2),
+                c_pairs[:].bitcast(I32).rearrange("p u n -> p n u")[:, cols],
             )
+
         c_code = sb.tile([P, N], U32, name="c_code", align_bytes=64)
-        c_scale = sb.tile([P, N], U8, name="c_scale", align_bytes=64)
+        c_scale = [
+            sb.tile([P, HALF], U8, name="c_scale0", align_bytes=64),
+            shared.tile([P, HALF], U8, name="c_scale1", offset=Q_RAW_AT, align_bytes=64),
+        ]
         q_code = sb.tile([P, NQ], U32, name="q_code", align_bytes=64)
         q_scale = sb.tile([P, NQ], U8, name="q_scale", align_bytes=64)
-        for h in range(2):
-            cols = slice(h * HALF, (h + 1) * HALF)
-            nc.vector.quantize_mx(out=c_code[:, cols].bitcast(FP8X4), scales=c_scale[:, cols], in_=c_bf[h][:])
 
+        def quantize_c(h):
+            nc.vector.quantize_mx(out=c_code[:, HALVES[h]].bitcast(FP8X4), scales=c_scale[h][:], in_=c_bf[h][:])
+
+        quantize_c(0)
         nc.vector.quantize_mx(
             out=q_code[:].bitcast(FP8X4), scales=q_scale[:], in_=q_bf[:].rearrange("p n t -> p (n t)")
         )
+        quantize_c(1)
+
+        k_code = sb.tile([P, N], U32, name="k_code", align_bytes=64)
+        for cols, entries in zip(HALVES, LIST_HALVES):
+            nc.vector.tensor_copy(k_code[:, cols], k_pool[:].bitcast(U32).indirect(k_list[:, entries]))
 
         def scores(bank, b, cols, code, scale):
+            rows = slice(b * P, (b + 1) * P)
             nc.tensor.matmul_mx(
                 out=bank[:, cols],
-                lhsT=q_code[:, b * P : (b + 1) * P].bitcast(FP8X4),
-                lhsT_scale=q_scale[:, b * P : (b + 1) * P],
+                lhsT=q_code[:, rows].bitcast(FP8X4),
+                lhsT_scale=q_scale[:, rows],
                 rhs=code[:, cols].bitcast(FP8X4),
-                rhs_scale=scale[:, cols],
+                rhs_scale=scale,
                 start=True,
                 stop=True,
             )
 
-        z_bank = [psum.tile([P, N], F32, name="z%d" % b) for b in range(2)]
-        a_bank = [psum.tile([P, N], F32, name="a%d" % b) for b in range(2)]
-        k_code = sb.tile([P, N], U32, name="k_code", align_bytes=64)
-        for h in range(2):
-            nc.vector.tensor_copy(
-                k_code[:, h * HALF : (h + 1) * HALF], k_pool[:].bitcast(U32).indirect(k_list[:, h * 16 : (h + 1) * 16])
-            )
-        halves = [slice(0, HALF), slice(HALF, N)]
-        for b, pieces in ((0, halves), (1, halves)):
-            for cols in pieces:
-                scores(z_bank[b], b, cols, c_code, c_scale)
-            for cols in pieces:
-                scores(a_bank[b], b, cols, k_code, k_scale)
+        z_bank = [psum.tile([P, N], F32, name="z%d" % b) for b in range(BLOCKS)]
+        a_bank = [psum.tile([P, N], F32, name="a%d" % b) for b in range(BLOCKS)]
+        for h, cols in enumerate(HALVES):
+            for b in range(BLOCKS):
+                scores(z_bank[b], b, cols, c_code, c_scale[h][:])
+        for cols in HALVES:
+            for b in range(BLOCKS):
+                scores(a_bank[b], b, cols, k_code, k_scale[:, cols])
 
+        def columns(name):
+            return [sb.tile([P, 1], F32, name="%s%d" % (name, b)) for b in range(BLOCKS)]
 
-        def col(name):
-            return sb.tile([P, 1], F32, name=name)
+        def wide(name):
+            return [sb.tile([P, N], F32, name="%s%d" % (name, b)) for b in range(BLOCKS)]
 
-        neg_t = [
-            late.tile([P, N + 1], F32, name="neg0", offset=0, align_bytes=64),
-            late.tile([P, N + 1], F32, name="neg1", offset=2240, align_bytes=64),
+        neg_mz = [
+            shared.tile([P, 1], F32, name="neg_mz%d" % b, offset=PICKED_AT + 64 * b, align_bytes=64)
+            for b in range(BLOCKS)
         ]
-        neg = [t[:] for t in neg_t]
-        e_z = [sb.tile([P, N], F32, name="e_z%d" % b) for b in range(2)]
-        e_a = [sb.tile([P, N], F32, name="e_a%d" % b) for b in range(2)]
-        l_z, l_a, neg_m, neg_h, total, inv = (
-            [col("%s%d" % (name, b)) for b in range(2)]
-            for name in ("l_z", "l_a", "neg_m", "neg_h", "total", "inv")
+        e_z, neg_a, e_a = wide("e_z"), wide("neg_a"), wide("e_a")
+        l_z, neg_m, shift, l_a, total, inv = (
+            columns(name) for name in ("l_z", "neg_m", "shift", "l_a", "total", "inv")
         )
-        shift = [col("shift%d" % b)[:] for b in range(2)]
-
-        def max_z(b):
-            neg_mz = neg[b][:, N : N + 1]
-            nc.vector.tensor_reduce(neg_mz, z_bank[b][:], mybir.AxisListType.X, ALU.max, negate=True)
-            nc.scalar.activation(e_z[b][:], z_bank[b][:], ACT.Exp, bias=neg_mz, accum_out=l_z[b][:])
-
-        def max_a(b, cols, start, result):
-            nc.vector.tensor_scalar(neg[b][:, cols], a_bank[b][:, cols], -1.0, start, ALU.mult, ALU.min, accum_out=result)
-
-        def exp_a(b):
-            nc.scalar.activation(shift[b], neg[b][:, N : N + 1], ACT.Exp, bias=neg_m[b][:], scale=-1.0)
-            nc.scalar.activation(e_a[b][:], neg[b][:, :N], ACT.Exp, bias=neg_m[b][:], scale=-1.0, accum_out=l_a[b][:])
+        for b in range(BLOCKS):
+            nc.vector.tensor_reduce(neg_mz[b][:], z_bank[b][:], mybir.AxisListType.X, ALU.max, negate=True)
+            nc.scalar.activation(e_z[b][:], z_bank[b][:], ACT.Exp, bias=neg_mz[b][:], accum_out=l_z[b][:])
+        for b in range(BLOCKS):
+            nc.vector.tensor_scalar(
+                neg_a[b][:], a_bank[b][:], -1.0, neg_mz[b][:], ALU.mult, ALU.min, accum_out=neg_m[b][:]
+            )
+            nc.scalar.activation(shift[b][:], neg_mz[b][:], ACT.Exp, bias=neg_m[b][:], scale=-1.0)
+            nc.scalar.activation(
+                e_a[b][:], neg_a[b][:], ACT.Exp, bias=neg_m[b][:], scale=-1.0, accum_out=l_a[b][:]
+            )
 
         def row_sum(b):
-            nc.vector.tensor_scalar(total[b][:], l_z[b][:], shift[b], l_a[b][:], ALU.mult, ALU.add)
+            nc.vector.tensor_scalar(total[b][:], l_z[b][:], shift[b][:], l_a[b][:], ALU.mult, ALU.add)
 
-        def invert(b):
-            nc.vector.reciprocal(inv[b][:], total[b][:])
+        def weights(b, cols):
+            y = sb.tile([P, cols.stop - cols.start], F32, name="y%d_%d" % (b, cols.start))
+            nc.vector.tensor_scalar(y[:], e_z[b][:, cols], shift[b][:], inv[b][:], ALU.mult, ALU.mult)
+            nc.sync.dma_start(out[0, b * P : (b + 1) * P, cols], y[:])
 
-        def weights(b, lo, hi, queue):
-            y = sb.tile([P, hi - lo], F32, name="y%d_%d" % (b, lo))
-            nc.vector.tensor_scalar(y[:], e_z[b][:, lo:hi], shift[b], inv[b][:], ALU.mult, ALU.mult)
-            queue.dma_start(out[0, b * P : (b + 1) * P, lo:hi], y[:])
-
-        max_z(0)
-        max_z(1)
-        max_a(0, slice(0, N), neg[0][:, N : N + 1], neg_m[0][:])
-        exp_a(0)
-        max_a(1, slice(0, N), neg[1][:, N : N + 1], neg_m[1][:])
-        exp_a(1)
         row_sum(0)
-        invert(0)
+        nc.vector.reciprocal(inv[0][:], total[0][:])
         row_sum(1)
-        weights(0, 0, N, nc.sync)
-        invert(1)
-        weights(1, 0, 256, nc.sync)
-        weights(1, 256, N, nc.scalar)
+        weights(0, slice(0, N))
+        nc.vector.reciprocal(inv[1][:], total[1][:])
+        for cols in HALVES:
+            weights(1, cols)

@@ -21,8 +21,8 @@ BLOCKS = NQ // P
 HALF = N // 2
 HALVES = (slice(0, HALF), slice(HALF, N))
 LIST_HALVES = (slice(0, HALF // 16), slice(HALF // 16, N // 16))
-CHUNK = TC // 2
-LAST_ON_VECTOR = 352
+ON_SCALAR = 96
+FIRST_ON_VECTOR = 704
 SCALE_FIRST, SCALE_STEP = 32, 4
 PICKED_AT, Q_RAW_AT = 0, 512
 
@@ -41,22 +41,29 @@ def tile_attend_locmix_topk_kernel(tc, qT, k_words, k_scales, cT, offs, offs2, o
         c_list = lists.tile([P, N // 16], U16, name="c_list")
         k_list = lists.tile([P, N // 16], U16, name="k_list")
         c_rows = cT.rearrange("(p t) n -> p t n", t=PACK)
-        c_raw = {}
-        for u in range(2):
-            for h in range(TC // CHUNK):
-                c_raw[u, h] = sb.tile([P, 2, CHUNK], F32, name="c_raw%d%d" % (u, h))
-                nc.sync.dma_start(c_raw[u, h][:], c_rows[:, 2 * u : 2 * u + 2, h * CHUNK : (h + 1) * CHUNK])
-                if (u, h) == (0, 0):
-                    nc.sync.dma_start(k_list[:], offs)
-                    nc.sync.dma_start(
-                        scale_pool[SCALE_FIRST : SCALE_FIRST + 16 * SCALE_STEP : SCALE_STEP, :],
-                        k_scales[0].bitcast(I32),
-                    )
-                    nc.sync.dma_start(c_list[:], offs2)
+        c_raw = [sb.tile([P, TC], F32, name="c_raw%d" % t, align_bytes=64) for t in range(PACK)]
+        for t in range(PACK):
+            nc.sync.dma_start(c_raw[t][:], c_rows[:, t, :])
+            if t == 0:
+                nc.sync.dma_start(c_list[:], offs2)
+                nc.sync.dma_start(k_list[:], offs)
+                nc.sync.dma_start(
+                    scale_pool[SCALE_FIRST : SCALE_FIRST + 16 * SCALE_STEP : SCALE_STEP, :],
+                    k_scales[0].bitcast(I32),
+                )
         q_raw = shared.tile([P, PACK, NQ], F32, name="q_raw", offset=Q_RAW_AT, align_bytes=64)
         nc.sync.dma_start(q_raw[:], qT[0].rearrange("(p t) n -> p t n", t=PACK))
         k_pool = sb.tile([P, T], I32, name="k_pool", align_bytes=64)
         nc.sync.dma_start(k_pool[:], k_words[0].rearrange("p n r -> p (n r)").bitcast(I32))
+
+        c_bf = sb.tile([P, N, PACK], BF16, name="c_bf", align_bytes=64)
+        row_bf = [sb.tile([P, TC], BF16, name="row_bf%d" % t, align_bytes=64) for t in range(2)]
+        for t in range(2):
+            cut = FIRST_ON_VECTOR if t == 0 else TC
+            nc.vector.tensor_copy(row_bf[t][:, :cut], c_raw[t][:, :cut])
+            if cut < TC:
+                nc.scalar.copy(row_bf[t][:, cut:], c_raw[t][:, cut:])
+            nc.scalar.activation(c_bf[:, :, t], row_bf[t][:].indirect(c_list[:]), ACT.Copy)
 
         picked = shared.tile([P, N], U8, name="picked", offset=PICKED_AT, align_bytes=64)
         nc.vector.tensor_copy(picked[:], scale_pool[:].bitcast(U8).indirect(k_list[:]))
@@ -70,51 +77,38 @@ def tile_attend_locmix_topk_kernel(tc, qT, k_words, k_scales, cT, offs, offs2, o
             )
         k_scale = k_scale_words[:].bitcast(U8)
 
-        c_pairs = sb.tile([P, 2, N], U32, name="c_pairs", align_bytes=64)
-        for u in range(2):
-            pair_pool = sb.tile([P, TC, 2], BF16, name="pair_pool%d" % u, align_bytes=64)
-            for h in range(TC // CHUNK):
-                src = c_raw[u, h][:].rearrange("p e n -> p n e")
-                dst = pair_pool[:, h * CHUNK : (h + 1) * CHUNK, :]
-                cut = LAST_ON_VECTOR if h == TC // CHUNK - 1 else 0
-                if cut:
-                    nc.vector.tensor_copy(dst[:, :cut, :], src[:, :cut, :])
-                nc.scalar.copy(dst[:, cut:, :], src[:, cut:, :])
-            window = pair_pool[:].rearrange("p n e -> p (n e)").bitcast(U32)
-            if u == 0:
-                nc.vector.tensor_copy(c_pairs[:, u, :], window.indirect(c_list[:]))
-            else:
-                for cols, entries in zip(HALVES, LIST_HALVES):
-                    nc.vector.tensor_copy(c_pairs[:, u, cols], window.indirect(c_list[:, entries]))
+        c_got = sb.tile([P, 2, N], F32, name="c_got", align_bytes=64)
+        nc.vector.tensor_copy(c_got[:, 0, :], c_raw[2][:].indirect(c_list[:]))
+        for cols, entries in zip(HALVES, LIST_HALVES):
+            nc.vector.tensor_copy(c_got[:, 1, cols], c_raw[3][:].indirect(c_list[:, entries]))
+        got = c_got[:].rearrange("p e n -> p n e")
+        nc.scalar.copy(c_bf[:, :ON_SCALAR, 2:], got[:, :ON_SCALAR, :])
+        nc.vector.tensor_copy(c_bf[:, ON_SCALAR:HALF, 2:], got[:, ON_SCALAR:HALF, :])
+        nc.vector.tensor_copy(c_bf[:, HALF:, 2:], got[:, HALF:, :])
 
         q_bf = sb.tile([P, NQ, PACK], BF16, name="q_bf", align_bytes=64)
         nc.scalar.copy(
             q_bf[:].rearrange("p (c i) t -> p c t i", i=4), q_raw[:].rearrange("p t (c i) -> p c t i", i=4)
         )
 
-        c_bf = [sb.tile([P, HALF * PACK], BF16, name="c_bf%d" % h, align_bytes=64) for h in range(2)]
-        for h, cols in enumerate(HALVES):
-            nc.vector.tensor_copy(
-                c_bf[h][:].bitcast(I32).rearrange("p (n u) -> p n u", u=2),
-                c_pairs[:].bitcast(I32).rearrange("p u n -> p n u")[:, cols],
-            )
-
         c_code = sb.tile([P, N], U32, name="c_code", align_bytes=64)
         c_scale = [
             sb.tile([P, HALF], U8, name="c_scale0", align_bytes=64),
-            shared.tile([P, HALF], U8, name="c_scale1", offset=Q_RAW_AT, align_bytes=64),
+            sb.tile([P, HALF], U8, name="c_scale1", align_bytes=64),
         ]
         q_code = sb.tile([P, NQ], U32, name="q_code", align_bytes=64)
         q_scale = sb.tile([P, NQ], U8, name="q_scale", align_bytes=64)
 
+        c_flat = c_bf[:].rearrange("p n t -> p (n t)")
+
         def quantize_c(h):
-            nc.vector.quantize_mx(out=c_code[:, HALVES[h]].bitcast(FP8X4), scales=c_scale[h][:], in_=c_bf[h][:])
+            nc.vector.quantize_mx(out=c_code[:, HALVES[h]].bitcast(FP8X4), scales=c_scale[h][:], in_=c_flat[:, h * HALF * PACK : (h + 1) * HALF * PACK])
 
         quantize_c(0)
+        quantize_c(1)
         nc.vector.quantize_mx(
             out=q_code[:].bitcast(FP8X4), scales=q_scale[:], in_=q_bf[:].rearrange("p n t -> p (n t)")
         )
-        quantize_c(1)
 
         k_code = sb.tile([P, N], U32, name="k_code", align_bytes=64)
         for cols, entries in zip(HALVES, LIST_HALVES):

@@ -21,10 +21,11 @@ BLOCKS = NQ // P
 HALF = N // 2
 HALVES = (slice(0, HALF), slice(HALF, N))
 LIST_HALVES = (slice(0, HALF // 16), slice(HALF // 16, N // 16))
-ON_SCALAR = 96
+ON_SCALAR = 128
 FIRST_ON_VECTOR = 704
 SCALE_FIRST, SCALE_STEP = 32, 4
-PICKED_AT, Q_RAW_AT = 0, 512
+NEG_A_AT = (0, 2112)
+PICKED_AT, Q_RAW_AT = 1856, 4224
 
 
 def tile_attend_locmix_topk_kernel(tc, qT, k_words, k_scales, cT, offs, offs2, out):
@@ -87,28 +88,32 @@ def tile_attend_locmix_topk_kernel(tc, qT, k_words, k_scales, cT, offs, offs2, o
         nc.vector.tensor_copy(c_bf[:, HALF:, 2:], got[:, HALF:, :])
 
         q_bf = sb.tile([P, NQ, PACK], BF16, name="q_bf", align_bytes=64)
-        nc.scalar.copy(
-            q_bf[:].rearrange("p (c i) t -> p c t i", i=4), q_raw[:].rearrange("p t (c i) -> p c t i", i=4)
-        )
+        for b in range(BLOCKS):
+            rows = slice(b * P, (b + 1) * P)
+            nc.scalar.copy(
+                q_bf[:, rows, :].rearrange("p (c i) t -> p c t i", i=4),
+                q_raw[:, :, rows].rearrange("p t (c i) -> p c t i", i=4),
+            )
 
         c_code = sb.tile([P, N], U32, name="c_code", align_bytes=64)
-        c_scale = [
-            sb.tile([P, HALF], U8, name="c_scale0", align_bytes=64),
-            sb.tile([P, HALF], U8, name="c_scale1", align_bytes=64),
-        ]
+        c_scale = sb.tile([P, N], U8, name="c_scale", align_bytes=64)
         q_code = sb.tile([P, NQ], U32, name="q_code", align_bytes=64)
         q_scale = sb.tile([P, NQ], U8, name="q_scale", align_bytes=64)
 
         c_flat = c_bf[:].rearrange("p n t -> p (n t)")
 
         def quantize_c(h):
-            nc.vector.quantize_mx(out=c_code[:, HALVES[h]].bitcast(FP8X4), scales=c_scale[h][:], in_=c_flat[:, h * HALF * PACK : (h + 1) * HALF * PACK])
+            nc.vector.quantize_mx(out=c_code[:, HALVES[h]].bitcast(FP8X4), scales=c_scale[:, HALVES[h]], in_=c_flat[:, h * HALF * PACK : (h + 1) * HALF * PACK])
 
         quantize_c(0)
         quantize_c(1)
-        nc.vector.quantize_mx(
-            out=q_code[:].bitcast(FP8X4), scales=q_scale[:], in_=q_bf[:].rearrange("p n t -> p (n t)")
-        )
+        for b in range(BLOCKS):
+            rows = slice(b * P, (b + 1) * P)
+            nc.vector.quantize_mx(
+                out=q_code[:, rows].bitcast(FP8X4),
+                scales=q_scale[:, rows],
+                in_=q_bf[:, rows, :].rearrange("p n t -> p (n t)"),
+            )
 
         k_code = sb.tile([P, N], U32, name="k_code", align_bytes=64)
         for cols, entries in zip(HALVES, LIST_HALVES):
@@ -128,9 +133,8 @@ def tile_attend_locmix_topk_kernel(tc, qT, k_words, k_scales, cT, offs, offs2, o
 
         z_bank = [psum.tile([P, N], F32, name="z%d" % b) for b in range(BLOCKS)]
         a_bank = [psum.tile([P, N], F32, name="a%d" % b) for b in range(BLOCKS)]
-        for h, cols in enumerate(HALVES):
-            for b in range(BLOCKS):
-                scores(z_bank[b], b, cols, c_code, c_scale[h][:])
+        for b in range(BLOCKS):
+            scores(z_bank[b], b, slice(0, N), c_code, c_scale[:])
         for cols in HALVES:
             for b in range(BLOCKS):
                 scores(a_bank[b], b, cols, k_code, k_scale[:, cols])
@@ -141,32 +145,35 @@ def tile_attend_locmix_topk_kernel(tc, qT, k_words, k_scales, cT, offs, offs2, o
         def wide(name):
             return [sb.tile([P, N], F32, name="%s%d" % (name, b)) for b in range(BLOCKS)]
 
-        neg_mz = [
-            shared.tile([P, 1], F32, name="neg_mz%d" % b, offset=PICKED_AT + 64 * b, align_bytes=64)
+        neg_a = [
+            shared.tile([P, N + 1], F32, name="neg_a%d" % b, offset=NEG_A_AT[b], align_bytes=64)
             for b in range(BLOCKS)
         ]
-        e_z, neg_a, e_a = wide("e_z"), wide("neg_a"), wide("e_a")
-        l_z, neg_m, shift, l_a, total, inv = (
-            columns(name) for name in ("l_z", "neg_m", "shift", "l_a", "total", "inv")
-        )
+        neg_mz = [neg_a[b][:, N:] for b in range(BLOCKS)]
+        e_z = wide("e_z")
+        e_a = [sb.tile([P, N + 1], F32, name="e_a%d" % b) for b in range(BLOCKS)]
+        shift = [e_a[b][:, N:] for b in range(BLOCKS)]
+        neg_m, l_a, total, inv = (columns(name) for name in ("neg_m", "l_a", "total", "inv"))
+        l_z = sb.tile([P, BLOCKS], F32, name="l_z")
+        l_z_less = sb.tile([P, BLOCKS], F32, name="l_z_less")
         for b in range(BLOCKS):
-            nc.vector.tensor_reduce(neg_mz[b][:], z_bank[b][:], mybir.AxisListType.X, ALU.max, negate=True)
-            nc.scalar.activation(e_z[b][:], z_bank[b][:], ACT.Exp, bias=neg_mz[b][:], accum_out=l_z[b][:])
+            nc.vector.tensor_reduce(neg_mz[b], z_bank[b][:], mybir.AxisListType.X, ALU.max, negate=True)
+            nc.scalar.activation(e_z[b][:], z_bank[b][:], ACT.Exp, bias=neg_mz[b], accum_out=l_z[:, b : b + 1])
         for b in range(BLOCKS):
             nc.vector.tensor_scalar(
-                neg_a[b][:], a_bank[b][:], -1.0, neg_mz[b][:], ALU.mult, ALU.min, accum_out=neg_m[b][:]
+                neg_a[b][:, :N], a_bank[b][:], -1.0, neg_mz[b], ALU.mult, ALU.min, accum_out=neg_m[b][:]
             )
-            nc.scalar.activation(shift[b][:], neg_mz[b][:], ACT.Exp, bias=neg_m[b][:], scale=-1.0)
             nc.scalar.activation(
                 e_a[b][:], neg_a[b][:], ACT.Exp, bias=neg_m[b][:], scale=-1.0, accum_out=l_a[b][:]
             )
+        nc.vector.tensor_scalar(l_z_less[:], l_z[:], -1.0, None, ALU.add)
 
         def row_sum(b):
-            nc.vector.tensor_scalar(total[b][:], l_z[b][:], shift[b][:], l_a[b][:], ALU.mult, ALU.add)
+            nc.vector.tensor_scalar(total[b][:], l_z_less[:, b : b + 1], shift[b], l_a[b][:], ALU.mult, ALU.add)
 
         def weights(b, cols):
             y = sb.tile([P, cols.stop - cols.start], F32, name="y%d_%d" % (b, cols.start))
-            nc.vector.tensor_scalar(y[:], e_z[b][:, cols], shift[b][:], inv[b][:], ALU.mult, ALU.mult)
+            nc.vector.tensor_scalar(y[:], e_z[b][:, cols], shift[b], inv[b][:], ALU.mult, ALU.mult)
             nc.sync.dma_start(out[0, b * P : (b + 1) * P, cols], y[:])
 
         row_sum(0)

@@ -22,6 +22,7 @@ HALF = N // 2
 HALVES = (slice(0, HALF), slice(HALF, N))
 LIST_HALVES = (slice(0, HALF // 16), slice(HALF // 16, N // 16))
 ON_SCALAR = 128
+FILL = 320
 FIRST_ON_VECTOR = 704
 SCALE_FIRST, SCALE_STEP = 32, 4
 NEG_A_AT = (0, 2112)
@@ -171,15 +172,21 @@ def tile_attend_locmix_topk_kernel(tc, qT, k_words, k_scales, cT, offs, offs2, o
         def row_sum(b):
             nc.vector.tensor_scalar(total[b][:], l_z_less[:, b : b + 1], shift[b], l_a[b][:], ALU.mult, ALU.add)
 
+        y = wide("y")
+
         def weights(b, cols):
-            y = sb.tile([P, cols.stop - cols.start], F32, name="y%d_%d" % (b, cols.start))
-            nc.vector.tensor_scalar(y[:], e_z[b][:, cols], shift[b], inv[b][:], ALU.mult, ALU.mult)
-            nc.sync.dma_start(out[0, b * P : (b + 1) * P, cols], y[:])
+            nc.vector.tensor_scalar(y[b][:, cols], e_z[b][:, cols], shift[b], inv[b][:], ALU.mult, ALU.mult)
+
+        def store(b, cols):
+            nc.sync.dma_start(out[0, b * P : (b + 1) * P, cols], y[b][:, cols])
 
         row_sum(0)
         nc.vector.reciprocal(inv[0][:], total[0][:])
         row_sum(1)
-        weights(0, slice(0, N))
+        weights(0, slice(0, FILL))
+        store(0, HALVES[0])
         nc.vector.reciprocal(inv[1][:], total[1][:])
-        for cols in HALVES:
-            weights(1, cols)
+        weights(0, slice(FILL, N))
+        store(0, HALVES[1])
+        weights(1, slice(0, N))
+        store(1, slice(0, N))

@@ -24,9 +24,10 @@ LIST_HALVES = (slice(0, HALF // 16), slice(HALF // 16, N // 16))
 ON_SCALAR = 128
 FILL = 320
 FIRST_ON_VECTOR = 704
+SECOND_ON_VECTOR = 224
 SCALE_FIRST, SCALE_STEP = 32, 4
 NEG_A_AT = (0, 2112)
-PICKED_AT, Q_RAW_AT = 1856, 4224
+PICKED_AT = 1856
 
 
 def tile_attend_locmix_topk_kernel(tc, qT, k_words, k_scales, cT, offs, offs2, out):
@@ -43,17 +44,19 @@ def tile_attend_locmix_topk_kernel(tc, qT, k_words, k_scales, cT, offs, offs2, o
         c_list = lists.tile([P, N // 16], U16, name="c_list")
         k_list = lists.tile([P, N // 16], U16, name="k_list")
         c_rows = cT.rearrange("(p t) n -> p t n", t=PACK)
-        c_raw = [sb.tile([P, TC], F32, name="c_raw%d" % t, align_bytes=64) for t in range(PACK)]
-        for t in range(PACK):
-            nc.sync.dma_start(c_raw[t][:], c_rows[:, t, :])
-            if t == 0:
-                nc.sync.dma_start(c_list[:], offs2)
-                nc.sync.dma_start(k_list[:], offs)
-                nc.sync.dma_start(
-                    scale_pool[SCALE_FIRST : SCALE_FIRST + 16 * SCALE_STEP : SCALE_STEP, :],
-                    k_scales[0].bitcast(I32),
-                )
-        q_raw = shared.tile([P, PACK, NQ], F32, name="q_raw", offset=Q_RAW_AT, align_bytes=64)
+        c_first = sb.tile([P, TC], F32, name="c_first", align_bytes=64)
+        c_middle = sb.tile([P, 2, TC], F32, name="c_middle", align_bytes=64)
+        c_last = sb.tile([P, TC], F32, name="c_last", align_bytes=64)
+        c_raw = [c_first[:], c_middle[:, 0, :], c_middle[:, 1, :], c_last[:]]
+        nc.sync.dma_start(c_first[:], c_rows[:, 0, :])
+        nc.sync.dma_start(c_list[:], offs2)
+        nc.sync.dma_start(k_list[:], offs)
+        nc.sync.dma_start(
+            scale_pool[SCALE_FIRST : SCALE_FIRST + 16 * SCALE_STEP : SCALE_STEP, :], k_scales[0].bitcast(I32)
+        )
+        nc.sync.dma_start(c_middle[:], c_rows[:, 1:3, :])
+        nc.sync.dma_start(c_last[:], c_rows[:, 3, :])
+        q_raw = sb.tile([P, PACK, NQ], F32, name="q_raw", align_bytes=64)
         nc.sync.dma_start(q_raw[:], qT[0].rearrange("(p t) n -> p t n", t=PACK))
         k_pool = sb.tile([P, T], I32, name="k_pool", align_bytes=64)
         nc.sync.dma_start(k_pool[:], k_words[0].rearrange("p n r -> p (n r)").bitcast(I32))
@@ -61,10 +64,9 @@ def tile_attend_locmix_topk_kernel(tc, qT, k_words, k_scales, cT, offs, offs2, o
         c_bf = sb.tile([P, N, PACK], BF16, name="c_bf", align_bytes=64)
         row_bf = [sb.tile([P, TC], BF16, name="row_bf%d" % t, align_bytes=64) for t in range(2)]
         for t in range(2):
-            cut = FIRST_ON_VECTOR if t == 0 else TC
+            cut = FIRST_ON_VECTOR if t == 0 else SECOND_ON_VECTOR
             nc.vector.tensor_copy(row_bf[t][:, :cut], c_raw[t][:, :cut])
-            if cut < TC:
-                nc.scalar.copy(row_bf[t][:, cut:], c_raw[t][:, cut:])
+            nc.scalar.copy(row_bf[t][:, cut:], c_raw[t][:, cut:])
             nc.scalar.activation(c_bf[:, :, t], row_bf[t][:].indirect(c_list[:]), ACT.Copy)
 
         picked = shared.tile([P, N], U8, name="picked", offset=PICKED_AT, align_bytes=64)
@@ -80,13 +82,12 @@ def tile_attend_locmix_topk_kernel(tc, qT, k_words, k_scales, cT, offs, offs2, o
         k_scale = k_scale_words[:].bitcast(U8)
 
         c_got = sb.tile([P, 2, N], F32, name="c_got", align_bytes=64)
-        nc.vector.tensor_copy(c_got[:, 0, :], c_raw[2][:].indirect(c_list[:]))
+        nc.vector.tensor_copy(c_got[:, 0, :], c_raw[2].indirect(c_list[:]))
         for cols, entries in zip(HALVES, LIST_HALVES):
-            nc.vector.tensor_copy(c_got[:, 1, cols], c_raw[3][:].indirect(c_list[:, entries]))
+            nc.vector.tensor_copy(c_got[:, 1, cols], c_raw[3].indirect(c_list[:, entries]))
         got = c_got[:].rearrange("p e n -> p n e")
-        nc.scalar.copy(c_bf[:, :ON_SCALAR, 2:], got[:, :ON_SCALAR, :])
-        nc.vector.tensor_copy(c_bf[:, ON_SCALAR:HALF, 2:], got[:, ON_SCALAR:HALF, :])
-        nc.vector.tensor_copy(c_bf[:, HALF:, 2:], got[:, HALF:, :])
+        for cols in HALVES:
+            nc.vector.tensor_copy(c_bf[:, cols, 2:], got[:, cols, :])
 
         q_bf = sb.tile([P, NQ, PACK], BF16, name="q_bf", align_bytes=64)
         for b in range(BLOCKS):
@@ -188,5 +189,6 @@ def tile_attend_locmix_topk_kernel(tc, qT, k_words, k_scales, cT, offs, offs2, o
         nc.vector.reciprocal(inv[1][:], total[1][:])
         weights(0, slice(FILL, N))
         store(0, HALVES[1])
-        weights(1, slice(0, N))
-        store(1, slice(0, N))
+        for cols in HALVES:
+            weights(1, cols)
+            store(1, cols)

@@ -26,8 +26,10 @@ FILL = 320
 FIRST_ON_VECTOR = 704
 SECOND_ON_VECTOR = 224
 SCALE_FIRST, SCALE_STEP = 32, 4
+QUARTER = N // 4
 NEG_A_AT = (0, 2112)
 PICKED_AT = 1856
+LAST_ROW_AT = 4224
 
 
 def tile_attend_locmix_topk_kernel(tc, qT, k_words, k_scales, cT, offs, offs2, out):
@@ -41,33 +43,44 @@ def tile_attend_locmix_topk_kernel(tc, qT, k_words, k_scales, cT, offs, offs2, o
         scale_pool = sb.tile([P, T // 4], I32, name="scale_pool", align_bytes=64)
         nc.vector.memset(scale_pool[:], 0)
 
+        q_raw = sb.tile([P, PACK, NQ], F32, name="q_raw", align_bytes=64)
+        nc.sync.dma_start(q_raw[:], qT[0].rearrange("(p t) n -> p t n", t=PACK))
         c_list = lists.tile([P, N // 16], U16, name="c_list")
         k_list = lists.tile([P, N // 16], U16, name="k_list")
-        c_rows = cT.rearrange("(p t) n -> p t n", t=PACK)
-        c_first = sb.tile([P, TC], F32, name="c_first", align_bytes=64)
-        c_middle = sb.tile([P, 2, TC], F32, name="c_middle", align_bytes=64)
-        c_last = sb.tile([P, TC], F32, name="c_last", align_bytes=64)
-        c_raw = [c_first[:], c_middle[:, 0, :], c_middle[:, 1, :], c_last[:]]
-        nc.sync.dma_start(c_first[:], c_rows[:, 0, :])
-        nc.sync.dma_start(c_list[:], offs2)
         nc.sync.dma_start(k_list[:], offs)
+        nc.sync.dma_start(c_list[:], offs2)
         nc.sync.dma_start(
             scale_pool[SCALE_FIRST : SCALE_FIRST + 16 * SCALE_STEP : SCALE_STEP, :], k_scales[0].bitcast(I32)
         )
-        nc.sync.dma_start(c_middle[:], c_rows[:, 1:3, :])
-        nc.sync.dma_start(c_last[:], c_rows[:, 3, :])
-        q_raw = sb.tile([P, PACK, NQ], F32, name="q_raw", align_bytes=64)
-        nc.sync.dma_start(q_raw[:], qT[0].rearrange("(p t) n -> p t n", t=PACK))
+        c_rows = cT.rearrange("(p t) n -> p t n", t=PACK)
+        c_pair = sb.tile([P, 2, TC], F32, name="c_pair", align_bytes=64)
+        c_late = [
+            sb.tile([P, TC], F32, name="c_late0", align_bytes=64),
+            shared.tile([P, TC], F32, name="c_late1", offset=LAST_ROW_AT, align_bytes=64),
+        ]
+        nc.sync.dma_start(c_pair[:], c_rows[:, :2, :])
+        for t in range(2):
+            nc.sync.dma_start(c_late[t][:], c_rows[:, 2 + t, :])
         k_pool = sb.tile([P, T], I32, name="k_pool", align_bytes=64)
         nc.sync.dma_start(k_pool[:], k_words[0].rearrange("p n r -> p (n r)").bitcast(I32))
 
-        c_bf = sb.tile([P, N, PACK], BF16, name="c_bf", align_bytes=64)
-        row_bf = [sb.tile([P, TC], BF16, name="row_bf%d" % t, align_bytes=64) for t in range(2)]
-        for t in range(2):
-            cut = FIRST_ON_VECTOR if t == 0 else SECOND_ON_VECTOR
-            nc.vector.tensor_copy(row_bf[t][:, :cut], c_raw[t][:, :cut])
-            nc.scalar.copy(row_bf[t][:, cut:], c_raw[t][:, cut:])
-            nc.scalar.activation(c_bf[:, :, t], row_bf[t][:].indirect(c_list[:]), ACT.Copy)
+        def planes(name, width):
+            code = [sb.tile([P, width], U32, name="%s_code%d" % (name, i), align_bytes=64) for i in range(2)]
+            scale = [sb.tile([P, width], U8, name="%s_scale%d" % (name, i), align_bytes=64) for i in range(2)]
+            return code, scale
+
+        def quantize(code, scale, values):
+            nc.vector.quantize_mx(
+                out=code[:].bitcast(FP8X4), scales=scale[:], in_=values[:].rearrange("p n t -> p (n t)")
+            )
+
+        q_bf = [sb.tile([P, P, PACK], BF16, name="q_bf%d" % b, align_bytes=64) for b in range(BLOCKS)]
+        for b in range(BLOCKS):
+            rows = slice(b * P, (b + 1) * P)
+            nc.scalar.copy(
+                q_bf[b][:].rearrange("p (c i) t -> p c t i", i=4),
+                q_raw[:, :, rows].rearrange("p t (c i) -> p c t i", i=4),
+            )
 
         picked = shared.tile([P, N], U8, name="picked", offset=PICKED_AT, align_bytes=64)
         nc.vector.tensor_copy(picked[:], scale_pool[:].bitcast(U8).indirect(k_list[:]))
@@ -81,53 +94,53 @@ def tile_attend_locmix_topk_kernel(tc, qT, k_words, k_scales, cT, offs, offs2, o
             )
         k_scale = k_scale_words[:].bitcast(U8)
 
-        c_got = sb.tile([P, 2, N], F32, name="c_got", align_bytes=64)
-        nc.vector.tensor_copy(c_got[:, 0, :], c_raw[2].indirect(c_list[:]))
-        for cols, entries in zip(HALVES, LIST_HALVES):
-            nc.vector.tensor_copy(c_got[:, 1, cols], c_raw[3].indirect(c_list[:, entries]))
-        got = c_got[:].rearrange("p e n -> p n e")
-        for cols in HALVES:
-            nc.vector.tensor_copy(c_bf[:, cols, 2:], got[:, cols, :])
-
-        q_bf = sb.tile([P, NQ, PACK], BF16, name="q_bf", align_bytes=64)
+        q_code, q_scale = planes("q", P)
         for b in range(BLOCKS):
-            rows = slice(b * P, (b + 1) * P)
-            nc.scalar.copy(
-                q_bf[:, rows, :].rearrange("p (c i) t -> p c t i", i=4),
-                q_raw[:, :, rows].rearrange("p t (c i) -> p c t i", i=4),
+            quantize(q_code[b], q_scale[b], q_bf[b])
+
+        c_bf = [sb.tile([P, HALF, PACK], BF16, name="c_bf%d" % h, align_bytes=64) for h in range(2)]
+        early = [sb.tile([P, 2, HALF], F32, name="early%d" % h, align_bytes=64) for h in range(2)]
+        for h, entries in enumerate(LIST_HALVES):
+            nc.scalar.activation(early[h][:, 0, :], c_pair[:, 0, :].indirect(c_list[:, entries]), ACT.Copy)
+            nc.vector.tensor_copy(early[h][:, 1, :], c_pair[:, 1, :].indirect(c_list[:, entries]))
+        for h in range(2):
+            nc.vector.tensor_copy(c_bf[h][:, :, :2], early[h][:].rearrange("p e n -> p n e"))
+
+        late = [sb.tile([P, 2, QUARTER], BF16, name="late%d" % i, align_bytes=64) for i in range(2)]
+        late_half = sb.tile([P, 2, HALF], BF16, name="late_half", align_bytes=64)
+        nc.vector.tensor_copy(late[0][:, 0, :], c_late[0][:].indirect(c_list[:, : QUARTER // 16]))
+        nc.scalar.activation(late[1][:, 0, :], c_late[0][:].indirect(c_list[:, QUARTER // 16 : HALF // 16]), ACT.Copy)
+        nc.scalar.activation(late_half[:, 0, :], c_late[0][:].indirect(c_list[:, LIST_HALVES[1]]), ACT.Copy)
+        for i in range(2):
+            entries = c_list[:, i * QUARTER // 16 : (i + 1) * QUARTER // 16]
+            nc.vector.tensor_copy(late[i][:, 1, :], c_late[1][:].indirect(entries))
+        nc.scalar.activation(late_half[:, 1, :], c_late[1][:].indirect(c_list[:, LIST_HALVES[1]]), ACT.Copy)
+        for i in range(2):
+            nc.vector.tensor_copy(
+                c_bf[0][:, i * QUARTER : (i + 1) * QUARTER, 2:], late[i][:].rearrange("p e n -> p n e")
             )
+        pairs = late_half[:].rearrange("p e n -> p n e")
+        nc.vector.tensor_copy(c_bf[1][:, :QUARTER, 2:], pairs[:, :QUARTER, :])
+        nc.scalar.copy(c_bf[1][:, QUARTER:, 2:], pairs[:, QUARTER:, :])
 
-        c_code = sb.tile([P, N], U32, name="c_code", align_bytes=64)
-        c_scale = sb.tile([P, N], U8, name="c_scale", align_bytes=64)
-        q_code = sb.tile([P, NQ], U32, name="q_code", align_bytes=64)
-        q_scale = sb.tile([P, NQ], U8, name="q_scale", align_bytes=64)
-
-        c_flat = c_bf[:].rearrange("p n t -> p (n t)")
-
-        def quantize_c(h):
-            nc.vector.quantize_mx(out=c_code[:, HALVES[h]].bitcast(FP8X4), scales=c_scale[:, HALVES[h]], in_=c_flat[:, h * HALF * PACK : (h + 1) * HALF * PACK])
-
-        quantize_c(0)
-        quantize_c(1)
-        for b in range(BLOCKS):
-            rows = slice(b * P, (b + 1) * P)
-            nc.vector.quantize_mx(
-                out=q_code[:, rows].bitcast(FP8X4),
-                scales=q_scale[:, rows],
-                in_=q_bf[:, rows, :].rearrange("p n t -> p (n t)"),
-            )
+        c_code = [
+            shared.tile([P, HALF], U32, name="c_code0", offset=LAST_ROW_AT, align_bytes=64),
+            sb.tile([P, HALF], U32, name="c_code1", align_bytes=64),
+        ]
+        c_scale = [sb.tile([P, HALF], U8, name="c_scale%d" % h, align_bytes=64) for h in range(2)]
+        for h in range(2):
+            quantize(c_code[h], c_scale[h], c_bf[h])
 
         k_code = sb.tile([P, N], U32, name="k_code", align_bytes=64)
         for cols, entries in zip(HALVES, LIST_HALVES):
             nc.vector.tensor_copy(k_code[:, cols], k_pool[:].bitcast(U32).indirect(k_list[:, entries]))
 
         def scores(bank, b, cols, code, scale):
-            rows = slice(b * P, (b + 1) * P)
             nc.tensor.matmul_mx(
                 out=bank[:, cols],
-                lhsT=q_code[:, rows].bitcast(FP8X4),
-                lhsT_scale=q_scale[:, rows],
-                rhs=code[:, cols].bitcast(FP8X4),
+                lhsT=q_code[b][:].bitcast(FP8X4),
+                lhsT_scale=q_scale[b][:],
+                rhs=code.bitcast(FP8X4),
                 rhs_scale=scale,
                 start=True,
                 stop=True,
@@ -135,11 +148,12 @@ def tile_attend_locmix_topk_kernel(tc, qT, k_words, k_scales, cT, offs, offs2, o
 
         z_bank = [psum.tile([P, N], F32, name="z%d" % b) for b in range(BLOCKS)]
         a_bank = [psum.tile([P, N], F32, name="a%d" % b) for b in range(BLOCKS)]
-        for b in range(BLOCKS):
-            scores(z_bank[b], b, slice(0, N), c_code, c_scale[:])
+        for h, cols in enumerate(HALVES):
+            for b in range(BLOCKS):
+                scores(z_bank[b], b, cols, c_code[h][:], c_scale[h][:])
         for cols in HALVES:
             for b in range(BLOCKS):
-                scores(a_bank[b], b, cols, k_code, k_scale[:, cols])
+                scores(a_bank[b], b, cols, k_code[:, cols], k_scale[:, cols])
 
         def columns(name):
             return [sb.tile([P, 1], F32, name="%s%d" % (name, b)) for b in range(BLOCKS)]
@@ -158,9 +172,13 @@ def tile_attend_locmix_topk_kernel(tc, qT, k_words, k_scales, cT, offs, offs2, o
         neg_m, l_a, total, inv = (columns(name) for name in ("neg_m", "l_a", "total", "inv"))
         l_z = sb.tile([P, BLOCKS], F32, name="l_z")
         l_z_less = sb.tile([P, BLOCKS], F32, name="l_z_less")
-        for b in range(BLOCKS):
+
+        def recent(b):
             nc.vector.tensor_reduce(neg_mz[b], z_bank[b][:], mybir.AxisListType.X, ALU.max, negate=True)
             nc.scalar.activation(e_z[b][:], z_bank[b][:], ACT.Exp, bias=neg_mz[b], accum_out=l_z[:, b : b + 1])
+
+        recent(0)
+        recent(1)
         for b in range(BLOCKS):
             nc.vector.tensor_scalar(
                 neg_a[b][:, :N], a_bank[b][:], -1.0, neg_mz[b], ALU.mult, ALU.min, accum_out=neg_m[b][:]

@@ -44,7 +44,7 @@ def tile_attend_locmix_topk_kernel(tc, qT, k_words, k_scales, cT, offs, offs2, o
         nc.vector.memset(scale_pool[:], 0)
 
         q_raw = sb.tile([P, PACK, NQ], F32, name="q_raw", align_bytes=64)
-        nc.sync.dma_start(q_raw[:], qT[0].rearrange("(p t) n -> p t n", t=PACK))
+        nc.scalar.dma_start(q_raw[:], qT[0].rearrange("(p t) n -> p t n", t=PACK))
         c_list = lists.tile([P, N // 16], U16, name="c_list")
         k_list = lists.tile([P, N // 16], U16, name="k_list")
         nc.sync.dma_start(k_list[:], offs)

@@ -168,45 +168,37 @@ def tile_attend_locmix_topk_kernel(tc, qT, k_words, k_scales, cT, offs, offs2, o
         neg_mz = [neg_a[b][:, N:] for b in range(BLOCKS)]
         e_z = wide("e_z")
         e_a = [sb.tile([P, N + 1], F32, name="e_a%d" % b) for b in range(BLOCKS)]
-        shift = [e_a[b][:, N:] for b in range(BLOCKS)]
-        neg_m, l_a, total, inv = (columns(name) for name in ("neg_m", "l_a", "total", "inv"))
-        l_z = sb.tile([P, BLOCKS], F32, name="l_z")
-        l_z_less = sb.tile([P, BLOCKS], F32, name="l_z_less")
+        neg_m, l_z = columns("neg_m"), columns("l_z")
+        tuples = [sb.tile([P, 6], F32, name="tuples%d" % b) for b in range(BLOCKS)]
+        for b in range(BLOCKS):
+            nc.vector.memset(tuples[b][:], 0.0)
+        l_a = [tuples[b][:, 0:1] for b in range(BLOCKS)]
+        l_z_shifted = [tuples[b][:, 3:4] for b in range(BLOCKS)]
+        shift = [tuples[b][:, 5:6] for b in range(BLOCKS)]
 
-        def recent(b):
+        for b in range(BLOCKS):
             nc.vector.tensor_reduce(neg_mz[b], z_bank[b][:], mybir.AxisListType.X, ALU.max, negate=True)
-            nc.scalar.activation(e_z[b][:], z_bank[b][:], ACT.Exp, bias=neg_mz[b], accum_out=l_z[:, b : b + 1])
-
-        recent(0)
-        recent(1)
+            nc.scalar.activation(e_z[b][:], z_bank[b][:], ACT.Exp, bias=neg_mz[b], accum_out=l_z[b][:])
         for b in range(BLOCKS):
             nc.vector.tensor_scalar(
                 neg_a[b][:, :N], a_bank[b][:], -1.0, neg_mz[b], ALU.mult, ALU.min, accum_out=neg_m[b][:]
             )
-            nc.scalar.activation(
-                e_a[b][:], neg_a[b][:], ACT.Exp, bias=neg_m[b][:], scale=-1.0, accum_out=l_a[b][:]
-            )
-        nc.vector.tensor_scalar(l_z_less[:], l_z[:], -1.0, None, ALU.add)
+            nc.scalar.activation(shift[b], neg_mz[b], ACT.Exp, bias=neg_m[b][:], scale=-1.0)
+            nc.scalar.activation(e_a[b][:], neg_a[b][:], ACT.Exp, bias=neg_m[b][:], scale=-1.0, accum_out=l_a[b])
 
-        def row_sum(b):
-            nc.vector.tensor_scalar(total[b][:], l_z_less[:, b : b + 1], shift[b], l_a[b][:], ALU.mult, ALU.add)
-
+        aggregate = [sb.tile([P, 2], F32, name="aggregate%d" % b) for b in range(BLOCKS)]
         y = wide("y")
 
-        def weights(b, cols):
-            nc.vector.tensor_scalar(y[b][:, cols], e_z[b][:, cols], shift[b], inv[b][:], ALU.mult, ALU.mult)
+        def shifted_sum(b):
+            nc.vector.tensor_scalar(l_z_shifted[b], l_z[b][:], -1.0, shift[b], ALU.add, ALU.mult)
 
-        def store(b, cols):
-            nc.sync.dma_start(out[0, b * P : (b + 1) * P, cols], y[b][:, cols])
+        def weights(b):
+            nc.vector.bn_aggr(aggregate[b][:], tuples[b][:])
+            for cols in HALVES:
+                nc.vector.tensor_scalar(y[b][:, cols], e_z[b][:, cols], aggregate[b][:, 1:], None, ALU.mult)
+                nc.sync.dma_start(out[0, b * P : (b + 1) * P, cols], y[b][:, cols])
 
-        row_sum(0)
-        nc.vector.reciprocal(inv[0][:], total[0][:])
-        row_sum(1)
-        weights(0, slice(0, FILL))
-        store(0, HALVES[0])
-        nc.vector.reciprocal(inv[1][:], total[1][:])
-        weights(0, slice(FILL, N))
-        store(0, HALVES[1])
-        for cols in HALVES:
-            weights(1, cols)
-            store(1, cols)
+        shifted_sum(0)
+        shifted_sum(1)
+        weights(0)
+        weights(1)

@@ -148,12 +148,12 @@ def tile_attend_locmix_topk_kernel(tc, qT, k_words, k_scales, cT, offs, offs2, o
 
         z_bank = [psum.tile([P, N], F32, name="z%d" % b) for b in range(BLOCKS)]
         a_bank = [psum.tile([P, N], F32, name="a%d" % b) for b in range(BLOCKS)]
-        for h, cols in enumerate(HALVES):
-            for b in range(BLOCKS):
+        for b in range(BLOCKS):
+            for h, cols in enumerate(HALVES):
                 scores(z_bank[b], b, cols, c_code[h][:], c_scale[h][:])
         for cols in HALVES:
-            for b in range(BLOCKS):
-                scores(a_bank[b], b, cols, k_code[:, cols], k_scale[:, cols])
+            scores(a_bank[0], 0, cols, k_code[:, cols], k_scale[:, cols])
+        scores(a_bank[1], 1, slice(0, N), k_code[:], k_scale)
 
         def columns(name):
             return [sb.tile([P, 1], F32, name="%s%d" % (name, b)) for b in range(BLOCKS)]

@@ -187,18 +187,27 @@ def tile_attend_locmix_topk_kernel(tc, qT, k_words, k_scales, cT, offs, offs2, o
             nc.scalar.activation(e_a[b][:], neg_a[b][:], ACT.Exp, bias=neg_m[b][:], scale=-1.0, accum_out=l_a[b])
 
         aggregate = [sb.tile([P, 2], F32, name="aggregate%d" % b) for b in range(BLOCKS)]
-        y = wide("y")
+        y_late = shared.tile([P, HALF], F32, name="y_late", offset=NEG_A_AT[1], align_bytes=64)
+        y = [
+            [sb.tile([P, HALF], F32, name="y00"), y_late],
+            [sb.tile([P, HALF], F32, name="y1%d" % h) for h in range(2)],
+        ]
 
         def shifted_sum(b):
             nc.vector.tensor_scalar(l_z_shifted[b], l_z[b][:], -1.0, shift[b], ALU.add, ALU.mult)
 
-        def weights(b):
+        def factor(b):
             nc.vector.bn_aggr(aggregate[b][:], tuples[b][:])
-            for cols in HALVES:
-                nc.vector.tensor_scalar(y[b][:, cols], e_z[b][:, cols], aggregate[b][:, 1:], None, ALU.mult)
-                nc.sync.dma_start(out[0, b * P : (b + 1) * P, cols], y[b][:, cols])
+
+        def weights(b, h):
+            nc.vector.tensor_scalar(y[b][h][:], e_z[b][:, HALVES[h]], aggregate[b][:, 1:], None, ALU.mult)
+            nc.sync.dma_start(out[0, b * P : (b + 1) * P, HALVES[h]], y[b][h][:])
 
         shifted_sum(0)
         shifted_sum(1)
-        weights(0)
-        weights(1)
+        factor(0)
+        weights(0, 0)
+        factor(1)
+        weights(0, 1)
+        weights(1, 0)
+        weights(1, 1)

@@ -21,11 +21,7 @@ BLOCKS = NQ // P
 HALF = N // 2
 HALVES = (slice(0, HALF), slice(HALF, N))
 LIST_HALVES = (slice(0, HALF // 16), slice(HALF // 16, N // 16))
-ON_SCALAR = 128
-FILL = 320
-FIRST_ON_VECTOR = 704
-SECOND_ON_VECTOR = 224
-SCALE_FIRST, SCALE_STEP = 32, 4
+SCALE_STEP = 8
 QUARTER = N // 4
 NEG_A_AT = (0, 2112)
 PICKED_AT = 1856
@@ -43,15 +39,14 @@ def tile_attend_locmix_topk_kernel(tc, qT, k_words, k_scales, cT, offs, offs2, o
         scale_pool = sb.tile([P, T // 4], I32, name="scale_pool", align_bytes=64)
         nc.vector.memset(scale_pool[:], 0)
 
-        q_raw = sb.tile([P, PACK, NQ], F32, name="q_raw", align_bytes=64)
-        nc.scalar.dma_start(q_raw[:], qT[0].rearrange("(p t) n -> p t n", t=PACK))
+        q_raw = [sb.tile([P, PACK, P], F32, name="q_raw%d" % b, align_bytes=64) for b in range(BLOCKS)]
+        for b in range(BLOCKS):
+            nc.scalar.dma_start(q_raw[b][:], qT[0].rearrange("(p t) n -> p t n", t=PACK)[:, :, b * P : (b + 1) * P])
         c_list = lists.tile([P, N // 16], U16, name="c_list")
         k_list = lists.tile([P, N // 16], U16, name="k_list")
         nc.sync.dma_start(k_list[:], offs)
         nc.sync.dma_start(c_list[:], offs2)
-        nc.sync.dma_start(
-            scale_pool[SCALE_FIRST : SCALE_FIRST + 16 * SCALE_STEP : SCALE_STEP, :], k_scales[0].bitcast(I32)
-        )
+        nc.sync.dma_start(scale_pool[0:P:SCALE_STEP, :], k_scales[0].bitcast(I32))
         c_rows = cT.rearrange("(p t) n -> p t n", t=PACK)
         c_pair = sb.tile([P, 2, TC], F32, name="c_pair", align_bytes=64)
         c_late = [
@@ -76,22 +71,17 @@ def tile_attend_locmix_topk_kernel(tc, qT, k_words, k_scales, cT, offs, offs2, o
 
         q_bf = [sb.tile([P, P, PACK], BF16, name="q_bf%d" % b, align_bytes=64) for b in range(BLOCKS)]
         for b in range(BLOCKS):
-            rows = slice(b * P, (b + 1) * P)
             nc.scalar.copy(
                 q_bf[b][:].rearrange("p (c i) t -> p c t i", i=4),
-                q_raw[:, :, rows].rearrange("p t (c i) -> p c t i", i=4),
+                q_raw[b][:].rearrange("p t (c i) -> p c t i", i=4),
             )
 
         picked = shared.tile([P, N], U8, name="picked", offset=PICKED_AT, align_bytes=64)
         nc.vector.tensor_copy(picked[:], scale_pool[:].bitcast(U8).indirect(k_list[:]))
         k_scale_words = sb.tile([P, N // 4], I32, name="k_scale_words", align_bytes=64)
-        nc.vector.memset(k_scale_words[:], 0)
-        for quad in range(4):
-            first = SCALE_FIRST + 4 * quad * SCALE_STEP
-            nc.sync.dma_start(
-                k_scale_words[32 * quad : 32 * quad + 4, :],
-                picked[:].bitcast(I32)[first : first + 4 * SCALE_STEP : SCALE_STEP, :],
-            )
+        nc.vector.tensor_copy(k_scale_words[:], picked[:].bitcast(I32))
+        for i in range(1, 4):
+            nc.sync.dma_start(k_scale_words[i:P:32, :], picked[:].bitcast(I32)[SCALE_STEP * i : P : 32, :])
         k_scale = k_scale_words[:].bitcast(U8)
 
         q_code, q_scale = planes("q", P)

@@ -19,13 +19,13 @@ P = 128
 PACK = 4
 BLOCKS = NQ // P
 HALF = N // 2
-HALVES = (slice(0, HALF), slice(HALF, N))
-LIST_HALVES = (slice(0, HALF // 16), slice(HALF // 16, N // 16))
-SCALE_STEP = 8
 QUARTER = N // 4
+HALVES = (slice(0, HALF), slice(HALF, N))
+SCALE_STEP = 8
 NEG_A_AT = (0, 2112)
 PICKED_AT = 1856
-LAST_ROW_AT = 4224
+Q_BF_AT = 4224
+C_BF_AT = 5248
 
 
 def tile_attend_locmix_topk_kernel(tc, qT, k_words, k_scales, cT, offs, offs2, out):
@@ -36,45 +36,28 @@ def tile_attend_locmix_topk_kernel(tc, qT, k_words, k_scales, cT, offs, offs2, o
         shared = ctx.enter_context(tc.tile_pool(name="shared", bufs=1))
         psum = ctx.enter_context(tc.psum_pool(name="psum", bufs=1))
 
+        c_rows = cT.rearrange("(p t) n -> p t n", t=PACK)
+        c_row = [sb.tile([P, TC], F32, name="c_row%d" % t, align_bytes=64) for t in range(PACK)]
+        nc.scalar.dma_start(c_row[0][:], c_rows[:, 0, :])
+
+        zeros = sb.tile([P, 16], F32, name="zeros")
+        nc.vector.memset(zeros[:], 0.0)
+        tuples = sb.tile([P, BLOCKS, 8], F32, name="tuples")
+        nc.scalar.copy(tuples[:].rearrange("p b j -> p (b j)"), zeros[:])
+
         scale_pool = sb.tile([P, T // 4], I32, name="scale_pool", align_bytes=64)
         nc.vector.memset(scale_pool[:], 0)
-
-        q_raw = [sb.tile([P, PACK, P], F32, name="q_raw%d" % b, align_bytes=64) for b in range(BLOCKS)]
-        for b in range(BLOCKS):
-            nc.scalar.dma_start(q_raw[b][:], qT[0].rearrange("(p t) n -> p t n", t=PACK)[:, :, b * P : (b + 1) * P])
         c_list = lists.tile([P, N // 16], U16, name="c_list")
         k_list = lists.tile([P, N // 16], U16, name="k_list")
         nc.sync.dma_start(k_list[:], offs)
         nc.sync.dma_start(c_list[:], offs2)
         nc.sync.dma_start(scale_pool[0:P:SCALE_STEP, :], k_scales[0].bitcast(I32))
-        c_rows = cT.rearrange("(p t) n -> p t n", t=PACK)
-        c_pair = sb.tile([P, 2, TC], F32, name="c_pair", align_bytes=64)
-        c_late = [
-            sb.tile([P, TC], F32, name="c_late0", align_bytes=64),
-            shared.tile([P, TC], F32, name="c_late1", offset=LAST_ROW_AT, align_bytes=64),
-        ]
-        nc.sync.dma_start(c_pair[:], c_rows[:, :2, :])
-        for t in range(2):
-            nc.sync.dma_start(c_late[t][:], c_rows[:, 2 + t, :])
+        for t in range(1, PACK):
+            nc.sync.dma_start(c_row[t][:], c_rows[:, t, :])
+        q_raw = sb.tile([P, PACK, NQ], F32, name="q_raw", align_bytes=64)
+        nc.sync.dma_start(q_raw[:], qT[0].rearrange("(p t) n -> p t n", t=PACK))
         k_pool = sb.tile([P, T], I32, name="k_pool", align_bytes=64)
         nc.sync.dma_start(k_pool[:], k_words[0].rearrange("p n r -> p (n r)").bitcast(I32))
-
-        def planes(name, width):
-            code = [sb.tile([P, width], U32, name="%s_code%d" % (name, i), align_bytes=64) for i in range(2)]
-            scale = [sb.tile([P, width], U8, name="%s_scale%d" % (name, i), align_bytes=64) for i in range(2)]
-            return code, scale
-
-        def quantize(code, scale, values):
-            nc.vector.quantize_mx(
-                out=code[:].bitcast(FP8X4), scales=scale[:], in_=values[:].rearrange("p n t -> p (n t)")
-            )
-
-        q_bf = [sb.tile([P, P, PACK], BF16, name="q_bf%d" % b, align_bytes=64) for b in range(BLOCKS)]
-        for b in range(BLOCKS):
-            nc.scalar.copy(
-                q_bf[b][:].rearrange("p (c i) t -> p c t i", i=4),
-                q_raw[b][:].rearrange("p t (c i) -> p c t i", i=4),
-            )
 
         picked = shared.tile([P, N], U8, name="picked", offset=PICKED_AT, align_bytes=64)
         nc.vector.tensor_copy(picked[:], scale_pool[:].bitcast(U8).indirect(k_list[:]))
@@ -84,50 +67,91 @@ def tile_attend_locmix_topk_kernel(tc, qT, k_words, k_scales, cT, offs, offs2, o
             nc.sync.dma_start(k_scale_words[i:P:32, :], picked[:].bitcast(I32)[SCALE_STEP * i : P : 32, :])
         k_scale = k_scale_words[:].bitcast(U8)
 
-        q_code, q_scale = planes("q", P)
-        for b in range(BLOCKS):
-            quantize(q_code[b], q_scale[b], q_bf[b])
+        def entries(first, count):
+            return slice(first // 16, (first + count) // 16)
 
-        c_bf = [sb.tile([P, HALF, PACK], BF16, name="c_bf%d" % h, align_bytes=64) for h in range(2)]
-        early = [sb.tile([P, 2, HALF], F32, name="early%d" % h, align_bytes=64) for h in range(2)]
-        for h, entries in enumerate(LIST_HALVES):
-            nc.scalar.activation(early[h][:, 0, :], c_pair[:, 0, :].indirect(c_list[:, entries]), ACT.Copy)
-            nc.vector.tensor_copy(early[h][:, 1, :], c_pair[:, 1, :].indirect(c_list[:, entries]))
-        for h in range(2):
-            nc.vector.tensor_copy(c_bf[h][:, :, :2], early[h][:].rearrange("p e n -> p n e"))
-
-        late = [sb.tile([P, 2, QUARTER], BF16, name="late%d" % i, align_bytes=64) for i in range(2)]
-        late_half = sb.tile([P, 2, HALF], BF16, name="late_half", align_bytes=64)
-        nc.vector.tensor_copy(late[0][:, 0, :], c_late[0][:].indirect(c_list[:, : QUARTER // 16]))
-        nc.scalar.activation(late[1][:, 0, :], c_late[0][:].indirect(c_list[:, QUARTER // 16 : HALF // 16]), ACT.Copy)
-        nc.scalar.activation(late_half[:, 0, :], c_late[0][:].indirect(c_list[:, LIST_HALVES[1]]), ACT.Copy)
-        for i in range(2):
-            entries = c_list[:, i * QUARTER // 16 : (i + 1) * QUARTER // 16]
-            nc.vector.tensor_copy(late[i][:, 1, :], c_late[1][:].indirect(entries))
-        nc.scalar.activation(late_half[:, 1, :], c_late[1][:].indirect(c_list[:, LIST_HALVES[1]]), ACT.Copy)
-        for i in range(2):
-            nc.vector.tensor_copy(
-                c_bf[0][:, i * QUARTER : (i + 1) * QUARTER, 2:], late[i][:].rearrange("p e n -> p n e")
-            )
-        pairs = late_half[:].rearrange("p e n -> p n e")
-        nc.vector.tensor_copy(c_bf[1][:, :QUARTER, 2:], pairs[:, :QUARTER, :])
-        nc.scalar.copy(c_bf[1][:, QUARTER:, 2:], pairs[:, QUARTER:, :])
-
-        c_code = [
-            shared.tile([P, HALF], U32, name="c_code0", offset=LAST_ROW_AT, align_bytes=64),
-            sb.tile([P, HALF], U32, name="c_code1", align_bytes=64),
+        piece = [
+            [sb.tile([P, 2, QUARTER], BF16, name="piece%d%d" % (e, i), align_bytes=64) for i in range(2)]
+            + [sb.tile([P, 2, HALF], BF16, name="piece%dh" % e, align_bytes=64)]
+            for e in range(2)
         ]
-        c_scale = [sb.tile([P, HALF], U8, name="c_scale%d" % h, align_bytes=64) for h in range(2)]
+        c_bf = [
+            sb.tile([P, HALF, PACK], BF16, name="c_bf0", align_bytes=64),
+            shared.tile([P, HALF, PACK], BF16, name="c_bf1", offset=C_BF_AT, align_bytes=64),
+        ]
+
+        def gather(engine, t, i):
+            first, count = (i * QUARTER, QUARTER) if i < 2 else (HALF, HALF)
+            window = c_row[t][:].indirect(c_list[:, entries(first, count)])
+            if engine == "vector":
+                nc.vector.tensor_copy(piece[t // 2][i][:, t % 2, :], window)
+            else:
+                nc.scalar.activation(piece[t // 2][i][:, t % 2, :], window, ACT.Copy)
+
+        def weave(engine, e, i):
+            places = slice(2 * e, 2 * e + 2)
+            target = c_bf[0][:, i * QUARTER : (i + 1) * QUARTER, places] if i < 2 else c_bf[1][:, :, places]
+            pairs = piece[e][i][:].rearrange("p e n -> p n e")
+            if engine == "vector":
+                nc.vector.tensor_copy(target, pairs)
+            else:
+                nc.scalar.copy(target, pairs)
+
+        for i in range(3):
+            gather("scalar", 0, i)
+        for i in range(2):
+            gather("vector", 1, i)
+        gather("scalar", 1, 2)
+        for i in range(3):
+            weave("vector", 0, i)
+        for i in range(3):
+            gather("scalar", 2, i)
+        for i in range(2):
+            gather("vector", 3, i)
+        gather("scalar", 3, 2)
+        for i in range(2):
+            weave("vector", 1, i)
+        weave("scalar", 1, 2)
+
+        q_bf = [
+            shared.tile([P, P, PACK], BF16, name="q_bf0", offset=Q_BF_AT, align_bytes=64),
+            sb.tile([P, P, PACK], BF16, name="q_bf1", align_bytes=64),
+        ]
+
+        def rounded(b):
+            return (
+                q_bf[b][:].rearrange("p (c i) t -> p c t i", i=4),
+                q_raw[:, :, b * P : (b + 1) * P].rearrange("p t (c i) -> p c t i", i=4),
+            )
+
+        nc.vector.tensor_copy(*rounded(0))
+        nc.scalar.copy(*rounded(1))
+
+        def quantize(code, scale, values):
+            nc.vector.quantize_mx(out=code.bitcast(FP8X4), scales=scale, in_=values[:].rearrange("p n t -> p (n t)"))
+
+        q_code = [sb.tile([P, P], U32, name="q_code%d" % b, align_bytes=64) for b in range(BLOCKS)]
+        q_scale = [
+            sb.tile([P, P], U8, name="q_scale0", align_bytes=64),
+            shared.tile([P, P], U8, name="q_scale1", offset=C_BF_AT, align_bytes=64),
+        ]
+        c_code = [sb.tile([P, HALF], U32, name="c_code%d" % h, align_bytes=64) for h in range(2)]
+        c_scale = [
+            shared.tile([P, HALF], U8, name="c_scale%d" % h, offset=Q_BF_AT + h * HALF, align_bytes=64)[:]
+            for h in range(2)
+        ]
+        quantize(q_code[0][:], q_scale[0][:], q_bf[0])
         for h in range(2):
-            quantize(c_code[h], c_scale[h], c_bf[h])
+            quantize(c_code[h][:], c_scale[h], c_bf[h])
+        quantize(q_code[1][:], q_scale[1][:], q_bf[1])
 
         k_code = sb.tile([P, N], U32, name="k_code", align_bytes=64)
-        for cols, entries in zip(HALVES, LIST_HALVES):
-            nc.vector.tensor_copy(k_code[:, cols], k_pool[:].bitcast(U32).indirect(k_list[:, entries]))
+        for h, cols in enumerate(HALVES):
+            nc.vector.tensor_copy(k_code[:, cols], k_pool[:].bitcast(U32).indirect(k_list[:, entries(h * HALF, HALF)]))
 
-        def scores(bank, b, cols, code, scale):
+        def scores(target, b, code, scale):
             nc.tensor.matmul_mx(
-                out=bank[:, cols],
+                out=target,
                 lhsT=q_code[b][:].bitcast(FP8X4),
                 lhsT_scale=q_scale[b][:],
                 rhs=code.bitcast(FP8X4),
@@ -136,39 +160,43 @@ def tile_attend_locmix_topk_kernel(tc, qT, k_words, k_scales, cT, offs, offs2, o
                 stop=True,
             )
 
-        z_bank = [psum.tile([P, N], F32, name="z%d" % b) for b in range(BLOCKS)]
+        z0_bank = [psum.tile([P, HALF], F32, name="z0%d" % h) for h in range(2)]
+        z1_bank = psum.tile([P, N], F32, name="z1")
         a_bank = [psum.tile([P, N], F32, name="a%d" % b) for b in range(BLOCKS)]
-        for b in range(BLOCKS):
-            for h, cols in enumerate(HALVES):
-                scores(z_bank[b], b, cols, c_code[h][:], c_scale[h][:])
+        for h in range(2):
+            scores(z0_bank[h][:], 0, c_code[h][:], c_scale[h])
+        for h, cols in enumerate(HALVES):
+            scores(z1_bank[:, cols], 1, c_code[h][:], c_scale[h])
         for cols in HALVES:
-            scores(a_bank[0], 0, cols, k_code[:, cols], k_scale[:, cols])
-        scores(a_bank[1], 1, slice(0, N), k_code[:], k_scale)
+            scores(a_bank[0][:, cols], 0, k_code[:, cols], k_scale[:, cols])
+        scores(a_bank[1][:], 1, k_code[:], k_scale)
 
         def columns(name):
             return [sb.tile([P, 1], F32, name="%s%d" % (name, b)) for b in range(BLOCKS)]
-
-        def wide(name):
-            return [sb.tile([P, N], F32, name="%s%d" % (name, b)) for b in range(BLOCKS)]
 
         neg_a = [
             shared.tile([P, N + 1], F32, name="neg_a%d" % b, offset=NEG_A_AT[b], align_bytes=64)
             for b in range(BLOCKS)
         ]
         neg_mz = [neg_a[b][:, N:] for b in range(BLOCKS)]
-        e_z = wide("e_z")
+        e_z = [sb.tile([P, N], F32, name="e_z%d" % b) for b in range(BLOCKS)]
         e_a = [sb.tile([P, N + 1], F32, name="e_a%d" % b) for b in range(BLOCKS)]
         neg_m, l_z = columns("neg_m"), columns("l_z")
-        tuples = [sb.tile([P, 6], F32, name="tuples%d" % b) for b in range(BLOCKS)]
-        for b in range(BLOCKS):
-            nc.vector.memset(tuples[b][:], 0.0)
-        l_a = [tuples[b][:, 0:1] for b in range(BLOCKS)]
-        l_z_shifted = [tuples[b][:, 3:4] for b in range(BLOCKS)]
-        shift = [tuples[b][:, 5:6] for b in range(BLOCKS)]
+        l_a = [tuples[:, b, 0:1] for b in range(BLOCKS)]
+        l_z_shifted = [tuples[:, b, 3:4] for b in range(BLOCKS)]
+        shift = [tuples[:, b, 5:6] for b in range(BLOCKS)]
 
-        for b in range(BLOCKS):
-            nc.vector.tensor_reduce(neg_mz[b], z_bank[b][:], mybir.AxisListType.X, ALU.max, negate=True)
-            nc.scalar.activation(e_z[b][:], z_bank[b][:], ACT.Exp, bias=neg_mz[b], accum_out=l_z[b][:])
+        neg_z0 = sb.tile([P, N], F32, name="neg_z0", align_bytes=64)
+        neg_half = sb.tile([P, 1], F32, name="neg_half")
+        nc.vector.tensor_scalar(
+            neg_z0[:, HALVES[0]], z0_bank[0][:], -1.0, None, ALU.mult, ALU.min, accum_out=neg_half[:]
+        )
+        nc.vector.tensor_scalar(
+            neg_z0[:, HALVES[1]], z0_bank[1][:], -1.0, neg_half[:], ALU.mult, ALU.min, accum_out=neg_mz[0]
+        )
+        nc.scalar.activation(e_z[0][:], neg_z0[:], ACT.Exp, bias=neg_mz[0], scale=-1.0, accum_out=l_z[0][:])
+        nc.vector.tensor_reduce(neg_mz[1], z1_bank[:], mybir.AxisListType.X, ALU.max, negate=True)
+        nc.scalar.activation(e_z[1][:], z1_bank[:], ACT.Exp, bias=neg_mz[1], accum_out=l_z[1][:])
         for b in range(BLOCKS):
             nc.vector.tensor_scalar(
                 neg_a[b][:, :N], a_bank[b][:], -1.0, neg_mz[b], ALU.mult, ALU.min, accum_out=neg_m[b][:]
@@ -187,7 +215,7 @@ def tile_attend_locmix_topk_kernel(tc, qT, k_words, k_scales, cT, offs, offs2, o
             nc.vector.tensor_scalar(l_z_shifted[b], l_z[b][:], -1.0, shift[b], ALU.add, ALU.mult)
 
         def factor(b):
-            nc.vector.bn_aggr(aggregate[b][:], tuples[b][:])
+            nc.vector.bn_aggr(aggregate[b][:], tuples[:, b, 0:6])
 
         def weights(b, h):
             nc.vector.tensor_scalar(y[b][h][:], e_z[b][:, HALVES[h]], aggregate[b][:, 1:], None, ALU.mult)

@@ -160,13 +160,11 @@ def tile_attend_locmix_topk_kernel(tc, qT, k_words, k_scales, cT, offs, offs2, o
                 stop=True,
             )
 
-        z0_bank = [psum.tile([P, HALF], F32, name="z0%d" % h) for h in range(2)]
-        z1_bank = psum.tile([P, N], F32, name="z1")
+        z_bank = [psum.tile([P, N], F32, name="z%d" % b) for b in range(BLOCKS)]
         a_bank = [psum.tile([P, N], F32, name="a%d" % b) for b in range(BLOCKS)]
-        for h in range(2):
-            scores(z0_bank[h][:], 0, c_code[h][:], c_scale[h])
-        for h, cols in enumerate(HALVES):
-            scores(z1_bank[:, cols], 1, c_code[h][:], c_scale[h])
+        for b in range(BLOCKS):
+            for h, cols in enumerate(HALVES):
+                scores(z_bank[b][:, cols], b, c_code[h][:], c_scale[h])
         for cols in HALVES:
             scores(a_bank[0][:, cols], 0, k_code[:, cols], k_scale[:, cols])
         scores(a_bank[1][:], 1, k_code[:], k_scale)
@@ -186,17 +184,9 @@ def tile_attend_locmix_topk_kernel(tc, qT, k_words, k_scales, cT, offs, offs2, o
         l_z_shifted = [tuples[:, b, 3:4] for b in range(BLOCKS)]
         shift = [tuples[:, b, 5:6] for b in range(BLOCKS)]
 
-        neg_z0 = sb.tile([P, N], F32, name="neg_z0", align_bytes=64)
-        neg_half = sb.tile([P, 1], F32, name="neg_half")
-        nc.vector.tensor_scalar(
-            neg_z0[:, HALVES[0]], z0_bank[0][:], -1.0, None, ALU.mult, ALU.min, accum_out=neg_half[:]
-        )
-        nc.vector.tensor_scalar(
-            neg_z0[:, HALVES[1]], z0_bank[1][:], -1.0, neg_half[:], ALU.mult, ALU.min, accum_out=neg_mz[0]
-        )
-        nc.scalar.activation(e_z[0][:], neg_z0[:], ACT.Exp, bias=neg_mz[0], scale=-1.0, accum_out=l_z[0][:])
-        nc.vector.tensor_reduce(neg_mz[1], z1_bank[:], mybir.AxisListType.X, ALU.max, negate=True)
-        nc.scalar.activation(e_z[1][:], z1_bank[:], ACT.Exp, bias=neg_mz[1], accum_out=l_z[1][:])
+        for b in range(BLOCKS):
+            nc.vector.tensor_reduce(neg_mz[b], z_bank[b][:], mybir.AxisListType.X, ALU.max, negate=True)
+            nc.scalar.activation(e_z[b][:], z_bank[b][:], ACT.Exp, bias=neg_mz[b], accum_out=l_z[b][:])
         for b in range(BLOCKS):
             nc.vector.tensor_scalar(
                 neg_a[b][:, :N], a_bank[b][:], -1.0, neg_mz[b], ALU.mult, ALU.min, accum_out=neg_m[b][:]

@@ -166,8 +166,8 @@ def tile_attend_locmix_topk_kernel(tc, qT, k_words, k_scales, cT, offs, offs2, o
             for h, cols in enumerate(HALVES):
                 scores(z_bank[b][:, cols], b, c_code[h][:], c_scale[h])
         for cols in HALVES:
-            scores(a_bank[0][:, cols], 0, k_code[:, cols], k_scale[:, cols])
-        scores(a_bank[1][:], 1, k_code[:], k_scale)
+            for b in range(BLOCKS):
+                scores(a_bank[b][:, cols], b, k_code[:, cols], k_scale[:, cols])
 
         def columns(name):
             return [sb.tile([P, 1], F32, name="%s%d" % (name, b)) for b in range(BLOCKS)]

@@ -24,8 +24,6 @@ HALVES = (slice(0, HALF), slice(HALF, N))
 SCALE_STEP = 8
 NEG_A_AT = (0, 2112)
 PICKED_AT = 1856
-Q_BF_AT = 4224
-C_BF_AT = 5248
 
 
 def tile_attend_locmix_topk_kernel(tc, qT, k_words, k_scales, cT, offs, offs2, out):
@@ -70,80 +68,51 @@ def tile_attend_locmix_topk_kernel(tc, qT, k_words, k_scales, cT, offs, offs2, o
         def entries(first, count):
             return slice(first // 16, (first + count) // 16)
 
-        piece = [
-            [sb.tile([P, 2, QUARTER], BF16, name="piece%d%d" % (e, i), align_bytes=64) for i in range(2)]
-            + [sb.tile([P, 2, HALF], BF16, name="piece%dh" % e, align_bytes=64)]
-            for e in range(2)
-        ]
-        c_bf = [
-            sb.tile([P, HALF, PACK], BF16, name="c_bf0", align_bytes=64),
-            shared.tile([P, HALF, PACK], BF16, name="c_bf1", offset=C_BF_AT, align_bytes=64),
-        ]
+        pair = [sb.tile([P, 2, N], BF16, name="pair%d" % e, align_bytes=64) for e in range(2)]
+        rounded = [sb.tile([P, HALF + P, PACK], BF16, name="rounded%d" % h, align_bytes=64) for h in range(2)]
 
-        def gather(engine, t, i):
-            first, count = (i * QUARTER, QUARTER) if i < 2 else (HALF, HALF)
-            window = c_row[t][:].indirect(c_list[:, entries(first, count)])
-            if engine == "vector":
-                nc.vector.tensor_copy(piece[t // 2][i][:, t % 2, :], window)
-            else:
-                nc.scalar.activation(piece[t // 2][i][:, t % 2, :], window, ACT.Copy)
+        def gather_views(t, first, count):
+            return pair[t // 2][:, t % 2, first : first + count], c_row[t][:].indirect(c_list[:, entries(first, count)])
 
-        def weave(engine, e, i):
-            places = slice(2 * e, 2 * e + 2)
-            target = c_bf[0][:, i * QUARTER : (i + 1) * QUARTER, places] if i < 2 else c_bf[1][:, :, places]
-            pairs = piece[e][i][:].rearrange("p e n -> p n e")
-            if engine == "vector":
-                nc.vector.tensor_copy(target, pairs)
-            else:
-                nc.scalar.copy(target, pairs)
-
-        for i in range(3):
-            gather("scalar", 0, i)
-        for i in range(2):
-            gather("vector", 1, i)
-        gather("scalar", 1, 2)
-        for i in range(3):
-            weave("vector", 0, i)
-        for i in range(3):
-            gather("scalar", 2, i)
-        for i in range(2):
-            gather("vector", 3, i)
-        gather("scalar", 3, 2)
-        for i in range(2):
-            weave("vector", 1, i)
-        weave("scalar", 1, 2)
-
-        q_bf = [
-            shared.tile([P, P, PACK], BF16, name="q_bf0", offset=Q_BF_AT, align_bytes=64),
-            sb.tile([P, P, PACK], BF16, name="q_bf1", align_bytes=64),
-        ]
-
-        def rounded(b):
+        def weave_views(e, first, count):
+            at = first % HALF
             return (
-                q_bf[b][:].rearrange("p (c i) t -> p c t i", i=4),
+                rounded[first // HALF][:, at : at + count, 2 * e : 2 * e + 2],
+                pair[e][:, :, first : first + count].rearrange("p e n -> p n e"),
+            )
+
+        nc.scalar.activation(*gather_views(0, 0, N), ACT.Copy)
+        nc.vector.tensor_copy(*gather_views(1, 0, HALF))
+        nc.scalar.activation(*gather_views(1, HALF, HALF), ACT.Copy)
+        for h in range(2):
+            nc.vector.tensor_copy(*weave_views(0, h * HALF, HALF))
+        nc.scalar.activation(*gather_views(2, 0, N), ACT.Copy)
+        for i in range(2):
+            nc.vector.tensor_copy(*gather_views(3, i * QUARTER, QUARTER))
+        nc.scalar.activation(*gather_views(3, HALF, HALF), ACT.Copy)
+        for i in range(3):
+            nc.vector.tensor_copy(*weave_views(1, i * QUARTER, QUARTER))
+        nc.scalar.copy(*weave_views(1, 3 * QUARTER, QUARTER))
+
+        def query_views(b):
+            return (
+                rounded[b][:, HALF:, :].rearrange("p (c i) t -> p c t i", i=4),
                 q_raw[:, :, b * P : (b + 1) * P].rearrange("p t (c i) -> p c t i", i=4),
             )
 
-        nc.vector.tensor_copy(*rounded(0))
-        nc.scalar.copy(*rounded(1))
+        nc.vector.tensor_copy(*query_views(0))
+        nc.scalar.copy(*query_views(1))
 
-        def quantize(code, scale, values):
-            nc.vector.quantize_mx(out=code.bitcast(FP8X4), scales=scale, in_=values[:].rearrange("p n t -> p (n t)"))
-
-        q_code = [sb.tile([P, P], U32, name="q_code%d" % b, align_bytes=64) for b in range(BLOCKS)]
-        q_scale = [
-            sb.tile([P, P], U8, name="q_scale0", align_bytes=64),
-            shared.tile([P, P], U8, name="q_scale1", offset=C_BF_AT, align_bytes=64),
-        ]
-        c_code = [sb.tile([P, HALF], U32, name="c_code%d" % h, align_bytes=64) for h in range(2)]
-        c_scale = [
-            shared.tile([P, HALF], U8, name="c_scale%d" % h, offset=Q_BF_AT + h * HALF, align_bytes=64)[:]
-            for h in range(2)
-        ]
-        quantize(q_code[0][:], q_scale[0][:], q_bf[0])
+        codes = [sb.tile([P, HALF + P], U32, name="codes%d" % h, align_bytes=64) for h in range(2)]
+        scales = [sb.tile([P, HALF + P], U8, name="scales%d" % h, align_bytes=64) for h in range(2)]
         for h in range(2):
-            quantize(c_code[h][:], c_scale[h], c_bf[h])
-        quantize(q_code[1][:], q_scale[1][:], q_bf[1])
+            nc.vector.quantize_mx(
+                out=codes[h][:].bitcast(FP8X4), scales=scales[h][:], in_=rounded[h][:].rearrange("p n t -> p (n t)")
+            )
+        q_code = [codes[b][:, HALF:] for b in range(BLOCKS)]
+        q_scale = [scales[b][:, HALF:] for b in range(BLOCKS)]
+        c_code = [codes[h][:, :HALF] for h in range(2)]
+        c_scale = [scales[h][:, :HALF] for h in range(2)]
 
         k_code = sb.tile([P, N], U32, name="k_code", align_bytes=64)
         for h, cols in enumerate(HALVES):
@@ -152,8 +121,8 @@ def tile_attend_locmix_topk_kernel(tc, qT, k_words, k_scales, cT, offs, offs2, o
         def scores(target, b, code, scale):
             nc.tensor.matmul_mx(
                 out=target,
-                lhsT=q_code[b][:].bitcast(FP8X4),
-                lhsT_scale=q_scale[b][:],
+                lhsT=q_code[b].bitcast(FP8X4),
+                lhsT_scale=q_scale[b],
                 rhs=code.bitcast(FP8X4),
                 rhs_scale=scale,
                 start=True,
@@ -164,7 +133,7 @@ def tile_attend_locmix_topk_kernel(tc, qT, k_words, k_scales, cT, offs, offs2, o
         a_bank = [psum.tile([P, N], F32, name="a%d" % b) for b in range(BLOCKS)]
         for b in range(BLOCKS):
             for h, cols in enumerate(HALVES):
-                scores(z_bank[b][:, cols], b, c_code[h][:], c_scale[h])
+                scores(z_bank[b][:, cols], b, c_code[h], c_scale[h])
         for cols in HALVES:
             for b in range(BLOCKS):
                 scores(a_bank[b][:, cols], b, k_code[:, cols], k_scale[:, cols])

from contextlib import ExitStack

import concourse.mybir as mybir

D, NQ, N, T, TC = 512, 256, 512, 2048, 1024
FLOPS = 2 * 2 * D * NQ * N

F32 = mybir.dt.float32
BF16 = mybir.dt.bfloat16
I32 = mybir.dt.int32
U32 = mybir.dt.uint32
U16 = mybir.dt.uint16
U8 = mybir.dt.uint8
FP8X4 = mybir.dt.float8_e4m3fn_x4
ALU = mybir.AluOpType
ACT = mybir.ActivationFunctionType

P = 128
PACK = 4
BLOCKS = NQ // P
HALF = N // 2
QUARTER = N // 4
HALVES = (slice(0, HALF), slice(HALF, N))
SCALE_STEP = 8
NEG_A_AT = (0, 2112)
PICKED_AT = 1856


def tile_attend_locmix_topk_kernel(tc, qT, k_words, k_scales, cT, offs, offs2, out):
    nc = tc.nc
    with ExitStack() as ctx:
        lists = ctx.enter_context(tc.tile_pool(name="lists", bufs=1))
        sb = ctx.enter_context(tc.tile_pool(name="sb", bufs=1))
        shared = ctx.enter_context(tc.tile_pool(name="shared", bufs=1))
        psum = ctx.enter_context(tc.psum_pool(name="psum", bufs=1))

        c_rows = cT.rearrange("(p t) n -> p t n", t=PACK)
        c_row = [sb.tile([P, TC], F32, name="c_row%d" % t, align_bytes=64) for t in range(PACK)]
        nc.scalar.dma_start(c_row[0][:], c_rows[:, 0, :])

        zeros = sb.tile([P, 16], F32, name="zeros")
        nc.vector.memset(zeros[:], 0.0)
        tuples = sb.tile([P, BLOCKS, 8], F32, name="tuples")
        nc.scalar.copy(tuples[:].rearrange("p b j -> p (b j)"), zeros[:])

        scale_pool = sb.tile([P, T // 4], I32, name="scale_pool", align_bytes=64)
        nc.vector.memset(scale_pool[:], 0)
        c_list = lists.tile([P, N // 16], U16, name="c_list")
        k_list = lists.tile([P, N // 16], U16, name="k_list")
        nc.sync.dma_start(k_list[:], offs)
        nc.sync.dma_start(c_list[:], offs2)
        nc.sync.dma_start(scale_pool[0:P:SCALE_STEP, :], k_scales[0].bitcast(I32))
        for t in range(1, PACK):
            nc.sync.dma_start(c_row[t][:], c_rows[:, t, :])
        q_raw = sb.tile([P, PACK, NQ], F32, name="q_raw", align_bytes=64)
        nc.sync.dma_start(q_raw[:], qT[0].rearrange("(p t) n -> p t n", t=PACK))
        k_pool = sb.tile([P, T], I32, name="k_pool", align_bytes=64)
        nc.sync.dma_start(k_pool[:], k_words[0].rearrange("p n r -> p (n r)").bitcast(I32))

        picked = shared.tile([P, N], U8, name="picked", offset=PICKED_AT, align_bytes=64)
        nc.vector.tensor_copy(picked[:], scale_pool[:].bitcast(U8).indirect(k_list[:]))
        k_scale_words = sb.tile([P, N // 4], I32, name="k_scale_words", align_bytes=64)
        nc.vector.tensor_copy(k_scale_words[:], picked[:].bitcast(I32))
        for i in range(1, 4):
            nc.sync.dma_start(k_scale_words[i:P:32, :], picked[:].bitcast(I32)[SCALE_STEP * i : P : 32, :])
        k_scale = k_scale_words[:].bitcast(U8)

        def entries(first, count):
            return slice(first // 16, (first + count) // 16)

        pair = [sb.tile([P, 2, N], BF16, name="pair%d" % e, align_bytes=64) for e in range(2)]
        rounded = [sb.tile([P, HALF + P, PACK], BF16, name="rounded%d" % h, align_bytes=64) for h in range(2)]

        def gather_views(t, first, count):
            return pair[t // 2][:, t % 2, first : first + count], c_row[t][:].indirect(c_list[:, entries(first, count)])

        def weave_views(e, first, count):
            at = first % HALF
            return (
                rounded[first // HALF][:, at : at + count, 2 * e : 2 * e + 2],
                pair[e][:, :, first : first + count].rearrange("p e n -> p n e"),
            )

        nc.scalar.activation(*gather_views(0, 0, N), ACT.Copy)
        nc.vector.tensor_copy(*gather_views(1, 0, HALF))
        nc.scalar.activation(*gather_views(1, HALF, HALF), ACT.Copy)
        for h in range(2):
            nc.vector.tensor_copy(*weave_views(0, h * HALF, HALF))
        nc.scalar.activation(*gather_views(2, 0, N), ACT.Copy)
        for i in range(2):
            nc.vector.tensor_copy(*gather_views(3, i * QUARTER, QUARTER))
        nc.scalar.activation(*gather_views(3, HALF, HALF), ACT.Copy)
        for i in range(3):
            nc.vector.tensor_copy(*weave_views(1, i * QUARTER, QUARTER))
        nc.scalar.copy(*weave_views(1, 3 * QUARTER, QUARTER))

        def query_views(b):
            return (
                rounded[b][:, HALF:, :].rearrange("p (c i) t -> p c t i", i=4),
                q_raw[:, :, b * P : (b + 1) * P].rearrange("p t (c i) -> p c t i", i=4),
            )

        nc.vector.tensor_copy(*query_views(0))
        nc.scalar.copy(*query_views(1))

        codes = [sb.tile([P, HALF + P], U32, name="codes%d" % h, align_bytes=64) for h in range(2)]
        scales = [sb.tile([P, HALF + P], U8, name="scales%d" % h, align_bytes=64) for h in range(2)]
        for h in range(2):
            nc.vector.quantize_mx(
                out=codes[h][:].bitcast(FP8X4), scales=scales[h][:], in_=rounded[h][:].rearrange("p n t -> p (n t)")
            )
        q_code = [codes[b][:, HALF:] for b in range(BLOCKS)]
        q_scale = [scales[b][:, HALF:] for b in range(BLOCKS)]
        c_code = [codes[h][:, :HALF] for h in range(2)]
        c_scale = [scales[h][:, :HALF] for h in range(2)]

        k_code = sb.tile([P, N], U32, name="k_code", align_bytes=64)
        for h, cols in enumerate(HALVES):
            nc.vector.tensor_copy(k_code[:, cols], k_pool[:].bitcast(U32).indirect(k_list[:, entries(h * HALF, HALF)]))

        def scores(target, b, code, scale):
            nc.tensor.matmul_mx(
                out=target,
                lhsT=q_code[b].bitcast(FP8X4),
                lhsT_scale=q_scale[b],
                rhs=code.bitcast(FP8X4),
                rhs_scale=scale,
                start=True,
                stop=True,
            )

        z_bank = [psum.tile([P, N], F32, name="z%d" % b) for b in range(BLOCKS)]
        a_bank = [psum.tile([P, N], F32, name="a%d" % b) for b in range(BLOCKS)]
        for b in range(BLOCKS):
            for h, cols in enumerate(HALVES):
                scores(z_bank[b][:, cols], b, c_code[h], c_scale[h])
        for cols in HALVES:
            for b in range(BLOCKS):
                scores(a_bank[b][:, cols], b, k_code[:, cols], k_scale[:, cols])

        def columns(name):
            return [sb.tile([P, 1], F32, name="%s%d" % (name, b)) for b in range(BLOCKS)]

        neg_a = [
            shared.tile([P, N + 1], F32, name="neg_a%d" % b, offset=NEG_A_AT[b], align_bytes=64)
            for b in range(BLOCKS)
        ]
        neg_mz = [neg_a[b][:, N:] for b in range(BLOCKS)]
        e_z = [sb.tile([P, N], F32, name="e_z%d" % b) for b in range(BLOCKS)]
        e_a = [sb.tile([P, N + 1], F32, name="e_a%d" % b) for b in range(BLOCKS)]
        neg_m, l_z = columns("neg_m"), columns("l_z")
        l_a = [tuples[:, b, 0:1] for b in range(BLOCKS)]
        l_z_shifted = [tuples[:, b, 3:4] for b in range(BLOCKS)]
        shift = [tuples[:, b, 5:6] for b in range(BLOCKS)]

        for b in range(BLOCKS):
            nc.vector.tensor_reduce(neg_mz[b], z_bank[b][:], mybir.AxisListType.X, ALU.max, negate=True)
            nc.scalar.activation(e_z[b][:], z_bank[b][:], ACT.Exp, bias=neg_mz[b], accum_out=l_z[b][:])
        for b in range(BLOCKS):
            nc.vector.tensor_scalar(
                neg_a[b][:, :N], a_bank[b][:], -1.0, neg_mz[b], ALU.mult, ALU.min, accum_out=neg_m[b][:]
            )
            nc.scalar.activation(shift[b], neg_mz[b], ACT.Exp, bias=neg_m[b][:], scale=-1.0)
            nc.scalar.activation(e_a[b][:], neg_a[b][:], ACT.Exp, bias=neg_m[b][:], scale=-1.0, accum_out=l_a[b])

        aggregate = [sb.tile([P, 2], F32, name="aggregate%d" % b) for b in range(BLOCKS)]
        y_late = shared.tile([P, HALF], F32, name="y_late", offset=NEG_A_AT[1], align_bytes=64)
        y = [
            [sb.tile([P, HALF], F32, name="y00"), y_late],
            [sb.tile([P, HALF], F32, name="y1%d" % h) for h in range(2)],
        ]

        def shifted_sum(b):
            nc.vector.tensor_scalar(l_z_shifted[b], l_z[b][:], -1.0, shift[b], ALU.add, ALU.mult)

        def factor(b):
            nc.vector.bn_aggr(aggregate[b][:], tuples[:, b, 0:6])

        def weights(b, h):
            nc.vector.tensor_scalar(y[b][h][:], e_z[b][:, HALVES[h]], aggregate[b][:, 1:], None, ALU.mult)
            nc.sync.dma_start(out[0, b * P : (b + 1) * P, HALVES[h]], y[b][h][:])

        shifted_sum(0)
        shifted_sum(1)
        factor(0)
        weights(0, 0)
        factor(1)
        weights(0, 1)
        weights(1, 0)
        weights(1, 1)
